import numpy as np, ml_dtypes
CORES = [8,136,40,168]
N = 4
BF = ml_dtypes.bfloat16
def gentries(a):
    return np.ascontiguousarray(a.reshape(8, 16, -1).transpose(0, 2, 1)).reshape(8, -1)
def gtable(e):
    e = np.asarray(e); return np.ascontiguousarray(e.reshape(8, -1, 16).transpose(0, 2, 1)).reshape(128, -1).astype(np.int32)
S, P, CAP, R = 8192, 2048, 768, 4
LEAST = -(-P // CAP)
def counts(rng, m):
    w = np.repeat(np.exp2(rng.integers(-2, 3, m)), CAP - 1); slot = np.argsort(-rng.random(m * (CAP - 1)) * w)[:P - m] // (CAP - 1)
    return np.bincount(slot, minlength=R) + (np.arange(R) < m)
def fountain(rng, cnt, src, e=1, full=False):
    pk = np.zeros((N, 128, P), np.float32); nb = np.zeros((N, 8, 4, P), np.int64)
    def pick(n):
        return np.minimum((rng.random(S) ** e * n).astype(np.int64), n - 1)
    for g in range(8):
        rd = np.concatenate([rng.permutation(np.repeat(np.arange(R), cnt[q, g])) for q in range(N)])
        at = np.argsort(rd, kind="stable"); t = rd[at]; end = np.concatenate([[0], np.cumsum(np.bincount(rd, minlength=R))])
        hi = end[t]; lo = end[np.maximum(t - 1, 0)]; most = np.maximum(hi, 3)
        a = lo + pick(np.maximum(hi - lo, 1))
        b = pick(most - 1); b = b + (b >= a)
        c = pick(most - 2); c = c + (c >= np.minimum(a, b)); c = c + (c >= np.maximum(a, b))
        if e > 1:
            o = np.concatenate([[S - 1, 0], 1 + rng.permutation(S - 2)])
        else:
            o = rng.permutation(S)
        deg = np.where(t == 0, 0, 3 if full else rng.integers(1, 4, S))
        row = np.stack([o, np.where(deg > 0, o[a], S), np.where(deg > 1, o[b], S), np.where(deg > 2, o[c], S)], axis=1)
        four = np.zeros((S, 4), np.int64); four[at] = rng.permuted(row, axis=1)
        v = np.concatenate([src[g], np.zeros((16, 1), np.int64)], axis=1)
        pk[:, 16 * g:16 * g + 16] = (np.sum(v[:, four], axis=2) & 255).reshape(16, N, P).transpose(1, 0, 2)
        nb[:, g] = four.reshape(N, P, 4).transpose(0, 2, 1)
    return {"packets": pk.astype(BF), "nb": np.stack([gtable(nb[q].reshape(8, 4 * P)) for q in range(N)])}
def anycounts(rng):
    return np.stack([np.stack([counts(rng, R) for g in range(8)]) for q in range(N)])
def setup_inputs(rng):
    return fountain(rng, anycounts(rng), rng.integers(0, 256, (8, 16, S)))
def setup_inputs_caps(rng):
    cnt = anycounts(rng); early = np.zeros(R, np.int64); early[:P // CAP] = CAP; early[P // CAP] = P % CAP
    for g in range(8):
        q = rng.permutation(N); cnt[q[0], g] = early; cnt[q[1], g] = early[::-1]
    cnt[:, rng.integers(0, 8)] = early
    return fountain(rng, cnt, rng.integers(0, 256, (8, 16, S)))
def setup_inputs_short(rng):
    m = rng.permutation(LEAST + np.arange(8) % (R - LEAST + 1)); cnt = np.stack([np.stack([counts(rng, m[g]) for g in range(8)]) for q in range(N)])
    return fountain(rng, cnt, rng.integers(0, 256, (8, 16, S)))
def setup_inputs_hubs(rng):
    return fountain(rng, anycounts(rng), rng.integers(236, 256, (8, 16, S)), e=8, full=True)
def setup_inputs_spread(rng):
    src = np.floor(rng.random((8, 16, S)) * np.exp2(rng.integers(0, 9, (8, 1, S)))) * (rng.random((8, 1, S)) > 0.0625)
    return fountain(rng, anycounts(rng), src.astype(np.int64))
def check_inputs(d):
    bad = []; x = d["packets"].astype(np.float32)
    if not ((x >= 0) & (x <= 255) & (x == np.floor(x))).all():
        bad.append("packets")
    if d["nb"].min() < 0 or d["nb"].max() > S:
        return bad + ["nb"]
    nbr = np.concatenate([gentries(d["nb"][q]).reshape(8, 4, P) for q in range(N)], axis=2).astype(np.int64)
    z = np.sort(nbr, axis=1)
    if ((z[:, 1:] == z[:, :-1]) & (z[:, 1:] < S)).any():
        bad.append("neighbours differ")
    known = np.zeros((8, S + 1), bool); known[:, S] = True; over = False
    for t in range(R):
        for g in range(8):
            un = ~known[g][nbr[g]]; j = np.nonzero(np.sum(un, axis=0) == 1)[0]
            over = over or np.bincount(j // P, minlength=N).max() > CAP
            known[g, np.sum(np.where(un[:, j], nbr[g][:, j], 0), axis=0)] = True
    if over:
        bad.append("cap")
    if not known.all():
        bad.append("all released")
    return bad
def reference(packets, nb):
    nbr = np.concatenate([gentries(nb[q]).reshape(8, 4, P) for q in range(N)], axis=2).astype(np.int64)
    pk = np.concatenate([packets[q].astype(np.float32).reshape(8, 16, P) for q in range(N)], axis=2).astype(np.int64)
    v = np.zeros((8, 16, S + 1), np.int64); known = np.zeros((8, S + 1), bool); known[:, S] = True
    w = np.zeros((8, S + 1), np.int64)
    for t in range(1, R + 1):
        for g in range(8):
            un = ~known[g][nbr[g]]; j = np.nonzero(np.sum(un, axis=0) == 1)[0]; p = nbr[g][:, j]
            s = np.sum(np.where(un[:, j], p, 0), axis=0)
            new = (pk[g][:, j] - np.sum(v[g][:, p], axis=1)) & 255
            v[g][:, s] = new; w[g, s] = t; known[g, s] = True
    y = v[:, :, :S].reshape(128, N, P).transpose(1, 0, 2); u = w[:, :S].reshape(8, N, P).transpose(1, 0, 2)
    return {"y": np.ascontiguousarray(y).astype(np.float32), "rounds": np.ascontiguousarray(u).astype(np.float32)}

@@ -1,0 +1,396 @@
+from concourse.bass import DstId, RemoteDMATransfer
+from concourse.mybir import AluOpType as ALU, AxisListType, ActivationFunctionType as ACT
+
+S, P, NR = 8192, 2048, 4
+M = 49152.0
+C = 16384.0
+E1 = 24576
+TW = S + 640
+WK = (-3.0, -1.5, -1.0, -0.5)
+LAM = (6.0, 3.0, 4.0, 5.0)
+CHUNKS = ((0, 0, 32), (1, 0, 32), (2, 0, 32), (3, 0, 32))
+RS = ()
+ORDER = "1q2d3"
+FL2 = 1
+START = (("n", (1,)), ("p", 1, 0, 512, False), ("n", (2, 3)), ("p", 2, 0, 512, False), ("p", 3, 0, 512, False))
+END = ((1, 0, 512, False), (2, 0, 512, False), (3, 0, 512, False))
+PK = [x[1:] for x in START if x[0] == "p"]
+
+SCRATCH = {"nbraw": ("sbuf", [128, 4, 128], "int32"), "nbs": ("sbuf", [128, 4, 4, 32], "uint16"),
+           "nbl": ("sbuf", [128, 4, 4, 32], "uint16"), "offs": ("sbuf", [128, 128], "uint16")}
+for _dt, _l in (("bfloat16", dict(pks=2048, pkl=2048, town=TW, tm=S + 16, gat=8192, qq=2048, rr=2048, ones=512, ident=128,
+                                  diag=512, wm=128, lfin=512, ext=2048, gm0=8, gm1=8, bsm=8, sg=384, ys=2048, yl=2048)),
+                ("int32", dict(p1=512, p2=512, p3=256, p4=128, p5=128, dum=64, pi0=4, pi1=4)),
+                ("float32", dict(nbc=512, gate=128, tt=512, scn=512, mk=4, bia=4, scl=4, wc=4, wp=4, wcol=1, rs=128, rl=128,
+                                 yf=2048))):
+    for _n in _l:
+        SCRATCH[_n] = ("sbuf", [128, _l[_n]], _dt)
+for _b in range(8):
+    SCRATCH["ps%d" % _b] = ("psum", [128, 512], "float32")
+
+SEMAPHORES = (["cv", "cs", "cp", "cg", "ldnb", "ldp0", "ldp1", "ldp2", "ldp3", "sent", "stored", "anb1", "anb2", "anb3", "ard"]
+              + ["apk%d" % _i for _i in range(8)] + ["ay%d" % _i for _i in range(8)])
+
+
+def relay_of(core, topo):
+    return [c for c in topo.cores_of(core) if topo.die(c) != topo.die(core)][0]
+
+
+def relay_program(g, core, owner, T, topo):
+    rank = T.rank_of(owner)
+    n = 0
+    for name, out, in_, plan in (("apk", T.pkl, T.pks, PK), ("ay", T.yl, T.ys, END)):
+        for i, (a, c0, c1, via) in enumerate(plan):
+            if via:
+                to = T.cores[(rank + a) % NR]
+                far = topo.engines(owner, to)
+                g.wait_ge(T.sem[name + str(i)], len([e for e in topo.engines(owner, core) if e not in far]))
+                rid, pid = topo.addr(to, core)
+                g.remote_dma(out[:, 512 * a + c0:512 * a + c1], in_[:, 512 * a + c0:512 * a + c1], T.sem[name + str(i)],
+                             T.sem.sent, pid, rid, topo.mask(core, to))
+                n += len(topo.engines(core, to))
+    if n:
+        g.wait_ge(T.sem.sent, n)
+
+
+def rank_program(g, core, T, topo):
+    rank = T.rank_of(core)
+    if rank is None:
+        for c in T.cores:
+            if relay_of(c, topo) == core:
+                relay_program(g, core, c, T, topo)
+        return
+    Q = {"v": g.vector, "s": g.scalar, "p": g.tensor, "g": g, "y": g.sync}
+    CS = {"v": "cv", "s": "cs", "p": "cp", "g": "cg"}
+    cnt = {"v": 0, "s": 0, "p": 0, "g": 0}
+    waited = {e: {} for e in Q}
+    wr, rd = {}, {}
+
+    def wait(e, tok):
+        if waited[e].get(tok[0], 0) < tok[1]:
+            Q[e].wait_ge(T.sem[tok[0]], tok[1])
+            waited[e][tok[0]] = tok[1]
+
+    def deps(e, reads, writes):
+        need = {}
+        for t in [t for r in reads for t in wr.get(r, [])] + [t for w in writes for t in wr.get(w, []) + rd.get(w, [])]:
+            need[t[0]] = max(need.get(t[0], 0), t[1])
+        for s in need:
+            if not (e == "p" and s == "cp"):
+                wait(e, (s, need[s]))
+
+    def op(e, fns, reads, writes):
+        if e == "g":
+            writes = writes + ["pool"]
+        deps(e, reads, writes)
+        ins = None
+        for f in (fns if isinstance(fns, list) else [fns]):
+            ins = f()
+        cnt[e] += 1
+        ins.then_inc(T.sem[CS[e]], 1)
+        tok = (CS[e], cnt[e])
+        for r in reads:
+            rd[r] = [t for t in rd.get(r, []) if t[0] != tok[0]] + [tok]
+        for w in writes:
+            wr[w] = [tok]
+            rd[w] = []
+
+    V, A, PE = g.vector, g.scalar, g.tensor
+    ps = [T["ps%d" % b] for b in range(8)]
+    peer = [T.cores[(rank + a) % NR] for a in range(NR)]
+    dst = [(rank + a) % NR for a in range(NR)]
+    src = [(rank - a) % NR for a in range(NR)]
+    relay = relay_of(core, topo)
+    far = topo.engines(core, peer[1])
+    near = [e for e in topo.engines(core, relay) if e not in far]
+    sent = [0]
+
+    def send(a, out, in_, sem, via, reads, lands):
+        deps("g", reads, [])
+        to, eng = (relay, near) if via else (peer[a], far)
+        rid, pid = topo.addr(to, core)
+        g.remote_dma(in_ if via else out, in_, T.sem[sem], T.sem.sent, pid, rid, sum(1 << e for e in eng))
+        sent[0] += len(eng)
+        wr[lands] = [(sem, len(far))]
+
+    def fused(slots, cut, outs, ins, sems, reads):
+        deps("g", reads, [])
+        trs = []
+        for i, a in enumerate(slots):
+            rid, pid = topo.addr(peer[a], core)
+            trs.append(RemoteDMATransfer(dst_ids=[DstId(rid=rid, pnc=pid)], dma_engine_mask=sum(1 << e for e in cut[i]),
+                                         remote_sem=T.sem[sems[i]], src=ins[i], dst=outs[i]))
+            sent[0] += len(cut[i])
+        g.remote_dma_fused(trs, local_sem=T.sem.sent)
+
+    def cuts(n):
+        h, q = len(far) // 2, len(far) // 4
+        return {1: [far], 2: [far[:h], far[h:]], 3: [far[:h], far[h:h + q], far[h + q:]]}[n]
+
+    g.sync.dma_start(T.nbraw[:], T.nb[:]).then_inc(T.sem.ldnb, 16)
+    wr["nbraw"] = [("ldnb", 16)]
+    seen = []
+    for a in [x[0] for x in PK][:2] + [0] + [x[0] for x in PK][2:]:
+        if a in seen:
+            continue
+        seen.append(a)
+        d = dst[a]
+        buf = T.pkl if a == 0 else T.pks
+        for j in range(4):
+            Q["sy"[j % 2]].dma_start(buf[32 * j:32 * j + 32, 512 * a:512 * a + 512],
+                                     T.packets[32 * d:32 * d + 32, 512 * j:512 * j + 512]).then_inc(T.sem["ldp%d" % a], 16)
+        wr[("pks", a)] = [("ldp%d" % a, 64)]
+
+    op("v", lambda: V.memset(T.town[:, 0:2048], M), [], [("to", 0)])
+    op("v", lambda: V.memset(T.ones[:], 1.0), [], ["ones"])
+    op("v", lambda: V.memset(T.town[:, 2048:4096], M), [], [("to", 1)])
+    op("s", lambda: A.activation(T.town[:, 4096:6144], T.town[:, 0:2048], ACT.Copy), [("to", 0)], [("to", 2)])
+    op("s", lambda: A.activation(T.town[:, 6144:8192], T.town[:, 0:2048], ACT.Copy), [("to", 0)], [("to", 3)])
+    op("s", [lambda b=b: A.activation(T.ext[:, 512 * b:512 * b + 512], T.ones[:], ACT.Copy, scale=0.0) for b in range(4)],
+       ["ones"], ["ext"])
+    TO = [("to", b) for b in range(4)]
+    op("g", lambda: g.iota(T.dum[:], [[0, 2], [16, 32]], S + E1, 1), [], ["dum"])
+    op("g", lambda: g.iota(T.pi0[:], [[-1, 4]], 16, 1), [], ["pi0"])
+
+    for a in (1, 2, 3, 0):
+        op("v", [lambda j=j: V.tensor_copy((T.nbs if a else T.nbl)[32 * j:32 * j + 32, a],
+                                           T.nbraw[32 * dst[a]:32 * dst[a] + 32, :, 32 * j:32 * j + 32])
+                 for j in range(4)], ["nbraw"], [("nbs" if a else "nbl", a)])
+    i = 0
+    for x in START:
+        if x[0] == "n":
+            cut = cuts(len(x[1]))
+            fused(x[1], cut, [T.nbl[:, a] for a in x[1]], [T.nbs[:, a] for a in x[1]], ["anb%d" % a for a in x[1]],
+                  [("nbs", a) for a in x[1]])
+            for k, a in enumerate(x[1]):
+                wr[("nbl", a)] = [("anb%d" % a, len(cut[k]))]
+        else:
+            a, c0, c1, via = x[1:]
+            send(a, T.pkl[:, 512 * a + c0:512 * a + c1], T.pks[:, 512 * a + c0:512 * a + c1], "apk%d" % i, via,
+                 [("pks", a)], ("pkl", i))
+            i += 1
+    wr[("pkl", "own")] = wr[("pks", 0)]
+    PKL = {a: [("pkl", i) for i, x in enumerate(PK) if x[0] == a] for a in (1, 2, 3)}
+    PKL[0] = [("pkl", "own")]
+
+    def single(a, b):
+        nb = [("nbl", x) for x in range(a, b)]
+        of = [("offs", x, c) for x in range(a, b) for c in range(0, 32, 8)]
+        op("v", lambda: V.tensor_scalar(T.p1[:, 128 * a:128 * b], T.nbl[:, a:b], E1, None, ALU.add), nb, [("p1", a)])
+        op("v", lambda: V.tensor_scalar(T.p2[:, 128 * a:128 * b], T.p1[:, 128 * a:128 * b], 32767, None, ALU.bitwise_and),
+           [("p1", a)], [("p2", a)])
+        op("v", [lambda x=x: V.tensor_tensor(T.p3[:, 64 * x:64 * x + 64], T.p2[:, 128 * x:128 * x + 64],
+                                             T.p2[:, 128 * x + 64:128 * x + 128], ALU.add) for x in range(a, b)],
+           [("p2", a)], [("p3", a)])
+        op("v", [lambda x=x: V.tensor_tensor(T.p4[:, 32 * x:32 * x + 32], T.p3[:, 64 * x:64 * x + 32],
+                                             T.p3[:, 64 * x + 32:64 * x + 64], ALU.add) for x in range(a, b)],
+           [("p3", a)], [("p4", a)])
+        op("v", lambda: V.tensor_tensor(T.p5[:, 32 * a:32 * b], T.p4[:, 32 * a:32 * b], T.dum[:, 0:32 * (b - a)], ALU.min),
+           [("p4", a), "dum"], [("p5", a)])
+        op("v", lambda: V.tensor_scalar(T.offs[:, 32 * a:32 * b], T.p5[:, 32 * a:32 * b], -float(E1), None, ALU.add), [("p5", a)], of)
+
+    def scatter1(a, c0, c1, key):
+        op("v", lambda: V.tensor_copy(T.town[:, 0:TW].indirect(T.offs[:, 32 * a + c0 // 16:32 * a + c1 // 16]),
+                                      T.pkl[:, 512 * a + c0:512 * a + c1]),
+           [("offs", a, c) for c in range(0, 32, 8)] + [key], TO)
+
+    single(0, 1)
+    scatter1(0, 0, 512, ("pkl", "own"))
+
+    op("g", lambda: g.affine_select(T.ident[:], T.ones[:, 0:128], [[-1, 128]], ALU.is_equal, 0.0, 0, 1), ["ones"], ["ident"])
+    op("g", lambda: g.affine_select(T.gm0[:], T.ones[:, 0:8], [[-16, 8]], ALU.is_ge, 0.0, 0, 1), ["ones"], ["gm0"])
+    op("g", lambda: g.affine_select(T.gm1[:], T.gm0[:], [[16, 8]], ALU.is_ge, 0.0, 15, -1), ["gm0"], ["gm1"])
+    for b in range(4):
+        op("g", lambda: g.affine_select(T.wm[32 * b:32 * b + 32, :], T.ones[32 * b:32 * b + 32, 0:128], [[0, 4], [-1, 32]],
+                                        ALU.is_equal, 0.0, 0, 1), ["ones"], ["wm"])
+    for b in range(4):
+        op("g", lambda: g.affine_select(T.lfin[32 * b:32 * b + 32, :], T.ones[32 * b:32 * b + 32, :], [[1, 4], [-1, 128]],
+                                        ALU.is_equal, 0.0, 0, 4), ["ones"], ["lfin"])
+    op("v", lambda: V.tensor_scalar(T.pi1[:], T.pi0[:], 15, None, ALU.bitwise_and), ["pi0"], ["pi1"])
+    op("v", [lambda k=k: V.memset(T.wc[:, k:k + 1], WK[k]) for k in range(4)], [], ["wc"])
+    op("v", lambda: V.tensor_scalar(T.mk[:], T.pi1[:], 0.0, None, ALU.is_equal), ["pi1"], ["mk"])
+    op("v", lambda: V.memset(T.gate[:], 0.0), [], ["gate"])
+    op("v", lambda: V.memset(T.tm[:, S:S + 16], 0.0), [], ["tmz"])
+    op("v", lambda: V.tensor_scalar(T.bia[:], T.mk[:], -256.0, None, ALU.mult), ["mk"], ["bia"])
+    op("v", lambda: V.tensor_tensor(T.wp[:], T.mk[:], T.wc[:], ALU.mult), ["mk", "wc"], ["wp"])
+    op("v", lambda: V.tensor_scalar(T.scl[:], T.mk[:], 2.0, -1.0, ALU.mult, ALU.add), ["mk"], ["scl"])
+    op("v", lambda: V.tensor_scalar(T.gate[:, 0:128:4], T.dum[:, 0:32], C - E1, None, ALU.add), ["dum"], ["gate"])
+    op("v", lambda: V.tensor_reduce(T.wcol[:], T.wp[:], AxisListType.X, ALU.add), ["wp"], ["wcol"])
+    op("s", lambda: A.activation(T.bsm[:], T.gm1[:], ACT.Identity, scale=T.wcol[:]), ["gm1", "wcol"], ["bsm"])
+    op("s", [lambda i=i: A.activation(T.ext[:, 129 * i:129 * i + 113:16], T.bsm[:], ACT.Copy) for i in range(16)], ["bsm"], ["ext"])
+    op("s", lambda: A.activation(T.diag[:, 0:128], T.ident[:], ACT.Copy, scale=-1.0), ["ident"], [("diag", 0)])
+    op("s", [lambda k=k: A.activation(T.diag[:, 128 * k:128 * k + 128], T.ident[:], ACT.Identity, scale=T.scl[:, k:k + 1])
+             for k in (1, 2, 3)], ["ident", "scl"], [("diag", 1)])
+
+    single(1, 2)
+    for i, (a, c0, c1, via) in enumerate(PK):
+        if i == 1:
+            single(2, 4)
+            op("v", [lambda k=k: V.tensor_scalar(T.nbc[:, k:512:4], T.nbl[:, :, k, :], C, None, ALU.add) for k in range(4)],
+               [("nbl", x) for x in range(4)], ["nbc"])
+        scatter1(a, c0, c1, ("pkl", i))
+
+    TM = [("tm", b) for b in range(16)] + ["tmz"]
+    bank = [0]
+
+    def merge():
+        for b in range(16):
+            k = bank[0] % 6
+            bank[0] += 1
+            op("p", lambda: PE.matmul(ps[k][:], T.wm[:], T.town[:, 512 * b:512 * b + 512], True, True), TO + ["wm"], [("ps", k)])
+            if b % 2 == 0:
+                op("s", lambda: A.activation(T.tm[:, 512 * b:512 * b + 512], ps[k][:], ACT.Identity, bias=-3 * M),
+                   [], [("ps", k), ("tm", b)])
+            else:
+                op("v", lambda: V.tensor_scalar(T.tm[:, 512 * b:512 * b + 512], ps[k][:], -3 * M, None, ALU.add),
+                   [], [("ps", k), ("tm", b)])
+
+    def flags(t, half):
+        fns = []
+        for a in (2 * half, 2 * half + 1):
+            d = dst[a]
+            for c in range(16):
+                o = 128 * t + 32 * a + c
+                fns.append(lambda o=o, d=d, c=c: PE.matmul(ps[7][:, o:o + 17:16], T.tm[:, P * d + c:P * d + P:16],
+                                                           T.ident[:, 0:17:16], True, True))
+        op("p", fns, TM + ["ident"], [("ps", 7)])
+
+    def peel(t):
+        n = len(CHUNKS)
+        win = T.tm[:, 0:S + 1]
+
+        def span(i):
+            a, c0, c1 = CHUNKS[i]
+            return a, c0, c1, 512 * a + 16 * c0, 16 * (c1 - c0)
+
+        def keys(name, i):
+            a, c0, c1 = CHUNKS[i]
+            return [(name, a, c) for c in range(c0, c1, 8)]
+
+        def gath(i, k):
+            a, c0, c1, u, w = span(i)
+            out = T.gat[:, P * k + u:P * k + u + w]
+            ind = win.indirect(T.nbl[:, a, k, c0:c1])
+            if k == 0:
+                op("v", lambda: V.tensor_copy(out, ind), TM + [("nbl", a)], keys(("g", k), i))
+            else:
+                op("s", lambda: A.activation(out, ind, ACT.Abs, bias=T.bia[:, k:k + 1]), TM + [("nbl", a), "bia"], keys(("g", k), i))
+
+        def gx(i, k):
+            if i == n:
+                return
+            gath(i, k)
+            a, c0, c1, u, w = span(i)
+            x = ps[i % 3][:, 0:w]
+            if k == 1:
+                op("p", lambda: PE.matmul(x, T.ident[:], T.pkl[:, u:u + w], True, False), PKL[a] + ["ident"], [("ps", i % 3)])
+            for kk in ((k,) if k != 2 else (0, 2)):
+                op("p", lambda: PE.matmul(x, T.diag[:, 128 * kk:128 * kk + 128], T.gat[:, P * kk + u:P * kk + u + w], False,
+                                          kk == 3 and i not in RS),
+                   keys(("g", kk), i) + [("diag", 0), ("diag", 1)], [("ps", i % 3)])
+
+        def quot(i):
+            a, c0, c1, u, w = span(i)
+            op("s", lambda: A.activation(T.qq[:, u:u + w], ps[i % 3][:, 0:w], ACT.Identity, bias=-127.5),
+               [], [("ps", i % 3)] + keys("q", i))
+            f = ps[3 + i % 2][:, 0:c1 - c0]
+            op("p", [lambda r=r: PE.matmul(f, T.ext[:, 128 * r:128 * r + 128], T.qq[:, u + r:u + w:16], r == 0, r == 15)
+                     for r in range(16)], keys("q", i) + ["ext"], [("ps", 3 + i % 2)])
+            if i in RS:
+                op("p", lambda: PE.matmul(ps[i % 3][:, 0:w], T.diag[:, 0:128], T.qq[:, u:u + w], False, True),
+                   keys("q", i), [("ps", i % 3)])
+
+        def dist(i):
+            a, c0, c1, u, w = span(i)
+            m = c1 - c0
+            op("s", [lambda k=k: A.activation(ps[5 + i % 2][:, k:4 * m:4], ps[3 + i % 2][:, 0:m], ACT.Abs, bias=-LAM[k] * M)
+                     for k in range(4)], [], [("ps", 3 + i % 2), ("ps", 5 + i % 2)])
+            if i in RS:
+                op("s", lambda: A.activation(T.rr[:, u:u + w], ps[i % 3][:, 0:w], ACT.Copy), [], [("ps", i % 3)] + keys("r", i))
+
+        def release(i):
+            a, c0, c1, u, w = span(i)
+            m = c1 - c0
+            o = 128 * a + 4 * c0
+            if i not in RS:
+                op("v", lambda: V.tensor_tensor(T.rr[:, u:u + w], ps[i % 3][:, 0:w], T.qq[:, u:u + w], ALU.subtract),
+                   keys("q", i), [("ps", i % 3)] + keys("r", i))
+            op("v", lambda: V.tensor_tensor(T.tt[:, o:o + 4 * m], ps[5 + i % 2][:, 0:4 * m], T.nbc[:, o:o + 4 * m], ALU.max),
+               ["nbc"], [("ps", 5 + i % 2)] + keys("t", i))
+            op("v", lambda: V.tensor_tensor_scan(T.scn[:, o:o + 4 * m], T.gate[:, 0:4 * m], T.tt[:, o:o + 4 * m], 0.0, ALU.max, ALU.min),
+               keys("t", i) + ["gate"], keys("sc", i))
+            of = T.offs[:, 32 * a + c0:32 * a + c1]
+            op("v", lambda: V.tensor_scalar(of, T.scn[:, o + 3:o + 4 * m:4], -C, None, ALU.add), keys("sc", i), keys("offs", i))
+            op("v", lambda: V.tensor_copy(T.town[:, 0:TW].indirect(of), T.rr[:, u:u + w]), keys("offs", i) + keys("r", i), TO)
+
+        flags(t - 2, 0)
+        for i in range(n):
+            gath(i, 0)
+        for k in (1, 2, 3):
+            gx(0, k)
+        for i in range(n):
+            for c in ORDER:
+                if c == "q":
+                    quot(i)
+                elif c == "d":
+                    dist(i)
+                else:
+                    gx(i + 1, int(c))
+            release(i)
+            if i == FL2:
+                flags(t - 2, 1)
+            if t == 4 and i == FL2 + 1:
+                rounds_out()
+
+    def rounds_out():
+        op("s", lambda: A.activation(T.sg[:], ps[7][:, 0:384], ACT.Sign, bias=-1000.0), [], [("ps", 7), "sg"])
+        op("p", [lambda t=t: PE.matmul(ps[7][:, 384:512], T.ident[:], T.sg[:, 128 * t:128 * t + 128], t == 0, t == 2)
+                 for t in range(3)], ["sg", "ident"], [("ps", 7)])
+        op("s", lambda: A.activation(T.rs[:], ps[7][:, 384:512], ACT.Identity, bias=2.5, scale=0.5), [], [("ps", 7), "rs"])
+        fused((1, 2, 3), cuts(3), [T.rl[:, 32 * a:32 * a + 32] for a in (1, 2, 3)], [T.rs[:, 32 * a:32 * a + 32] for a in (1, 2, 3)],
+              ["ard"] * 3, ["rs"])
+        wr["rl"] = [("ard", len(far))]
+
+    merge()
+    peel(2)
+    merge()
+    peel(3)
+    merge()
+    peel(4)
+
+    stored = [0]
+
+    def store(e, out, in_, reads):
+        deps(e, reads, [])
+        Q[e].dma_start(out, in_).then_inc(T.sem.stored, 16)
+        stored[0] += 16
+
+    for a in range(4):
+        for h in range(2):
+            buf = T.rs if a == 0 else T.rl
+            store("y", T.rounds[2 * src[a] + h], buf[:, 32 * a + 16 * h:32 * a + 16 * h + 16], ["rs" if a == 0 else "rl"])
+    for i, (a, c0, c1, via) in enumerate(list(END) + [(0, 0, 512, False)]):
+        k = i % 6
+        w = c1 - c0
+        o = P * dst[a] + 4 * c0
+        op("p", [lambda j=j: PE.matmul(ps[k][:, 0:w], T.lfin[:, 128 * j:128 * j + 128], T.town[:, o + w * j:o + w * j + w],
+                                       j == 0, j == 3) for j in range(4)], TO + ["lfin"], [("ps", k)])
+        out = T.yf[:, 0:512] if a == 0 else T.ys[:, 512 * a + c0:512 * a + c1]
+        if i % 2 == 0:
+            op("v", lambda: V.tensor_scalar(out, ps[k][:, 0:w], -3 * M, None, ALU.add), [], [("ps", k), ("ys", i)])
+        else:
+            op("s", lambda: A.activation(out, ps[k][:, 0:w], ACT.Identity, bias=-3 * M), [], [("ps", k), ("ys", i)])
+        if a:
+            send(a, T.yl[:, 512 * a + c0:512 * a + c1], out, "ay%d" % i, via, [("ys", i)], ("yl", i))
+        else:
+            store("s", T.y[32 * rank:32 * rank + 32, :], out, [("ys", i)])
+    for i, (a, c0, c1, via) in sorted(enumerate(END), key=lambda x: x[1][3]):
+        o = 512 * a + c0
+        h = (c1 - c0) // 2
+        op("v", lambda: V.tensor_copy(T.yf[:, o:o + h], T.yl[:, o:o + h]), [("yl", i)], [("yf", i, 0)])
+        op("s", lambda: A.activation(T.yf[:, o + h:o + 2 * h], T.yl[:, o + h:o + 2 * h], ACT.Copy), [("yl", i)], [("yf", i, 1)])
+        store("y", T.y[32 * src[a]:32 * src[a] + 32, 4 * c0:4 * c1], T.yf[:, o:o + 2 * h], [("yf", i, 0), ("yf", i, 1)])
+    g.sync.wait_ge(T.sem.stored, stored[0])
+    g.wait_ge(T.sem.sent, sent[0])
+    for e in cnt:
+        wait("g", (CS[e], cnt[e]))

@@ -1,64 +1,51 @@
 from concourse.bass import DstId, RemoteDMATransfer
-from concourse.mybir import AluOpType as ALU, AxisListType, ActivationFunctionType as ACT
+from concourse.mybir import AluOpType as ALU, ActivationFunctionType as ACT
 
-S, P, NR = 8192, 2048, 4
-M = 49152.0
+S, P, NR, CAP = 8192, 2048, 4, 768
+M, M0 = 61440.0, 24576.0
+X, X0 = 96256.0, 61440.0
 C = 16384.0
-E1 = 24576
-TW = S + 640
-WK = (-3.0, -1.5, -1.0, -0.5)
-LAM = (6.0, 3.0, 4.0, 5.0)
-CHUNKS = ((0, 0, 32), (1, 0, 32), (2, 0, 32), (3, 0, 32))
-RS = ()
-ORDER = "1q2d3"
-FL2 = 1
-START = (("n", (1,)), ("p", 1, 0, 512, False), ("n", (2, 3)), ("p", 2, 0, 512, False), ("p", 3, 0, 512, False))
-END = ((1, 0, 512, False), (2, 0, 512, False), (3, 0, 512, False))
-PK = [x[1:] for x in START if x[0] == "p"]
+E1 = 3 * S + 32768
+CB = S + 640
+DB = CB + CAP
+TW = DB + 640
+BIG = 2048.0
+WK = (-3.0, -1.0, 1.0, 3.0, 7.0)
+LAM = [7 * (X - M - 384) + w * M0 for w in WK[:4]]
+TWO = 134000.0
+FULL = ((0, 32), (32, 64), (64, 96), (96, 128))
+ROUND = {
+    2: (FULL, "n0 11 30 w0 20 v0 w2 e0 01 x1 y3 q0 y2 y1 r0 22 e1 d0 a0 Q1 02 13 03 d1 q2 b0 c0 r1 s0 a1 r2 23 b1 d2 q3 c1 a2 z3 s1 d3 b2 a3 c2 b3 s2 r3 c3 e2 s3"),
+    3: (FULL, "x0 30 v0 x1 10 11 y1 q0 v1 22 v2 r0 d0 p0 a0 z1 q1 b0 12 32 33 d1 z2 c0 s0 p1 q2 23 r1 a1 b1 c1 s1 13 03 r2 d2 p2 q3 a2 z3 b2 c2 d3 s2 p3 a3 r3 b3 c3 s3"),
+    4: (((0, 28), (28, 48)), "u0 10 v0 30 x0 x1 01 w1 q0 y1 z1 n0 r0 d0 q1 a0 d1 b0 r1 c0 s0 a1 b1 o0 c1 o1 s1"),
+}
+LAST = ((3, 8, 10, 14, 15), "svsvsvsvsvvvsvsv")
+TURNS = (("n", 0), ("n", 1), ("p", 0), ("p", 1), ("n", 2), ("n", 3), ("p", 2), ("p", 3))
+LOADS = (("p", 1), ("n", 1), ("n", 2), ("n", 3), ("n", 0), ("p", 2), ("p", 0), ("p", 3))
 
-SCRATCH = {"nbraw": ("sbuf", [128, 4, 128], "int32"), "nbs": ("sbuf", [128, 4, 4, 32], "uint16"),
-           "nbl": ("sbuf", [128, 4, 4, 32], "uint16"), "offs": ("sbuf", [128, 128], "uint16")}
-for _dt, _l in (("bfloat16", dict(pks=2048, pkl=2048, town=TW, tm=S + 16, gat=8192, qq=2048, rr=2048, ones=512, ident=128,
-                                  diag=512, wm=128, lfin=512, ext=2048, gm0=8, gm1=8, bsm=8, sg=384, ys=2048, yl=2048)),
-                ("int32", dict(p1=512, p2=512, p3=256, p4=128, p5=128, dum=64, pi0=4, pi1=4)),
-                ("float32", dict(nbc=512, gate=128, tt=512, scn=512, mk=4, bia=4, scl=4, wc=4, wp=4, wcol=1, rs=128, rl=128,
-                                 yf=2048))):
+SCRATCH = {"ys": ("sbuf", [128, 4, 544], "bfloat16"), "yl": ("sbuf", [128, 4, 544], "bfloat16"),
+           "nbq": ("sbuf", [128, 4, 128], "int32"), "nbs": ("sbuf", [128, 4, 160], "uint16"),
+           "nbl": ("sbuf", [128, 4, 160], "uint16"), "nbr": ("sbuf", [128, 4, 128], "uint16"),
+           "nb4": ("sbuf", [128, 5, 48], "uint16"), "offs": ("sbuf", [128, 128], "uint16"),
+           "dig": ("sbuf", [128, 10, 128], "bfloat16"), "zz": ("sbuf", [128, 6, 144], "bfloat16")}
+for _dt, _l in (("bfloat16", dict(pks=2048, pkl=2048, pkr=2048, pk4=CAP, town=TW, tm=S + 16, gat=8192, qq=2048, rr=2048, ones=512,
+                                  ident=128, diag=768, wm=128, lfin=512, sg=384, fl=384, pay0=2048, pay=2048,
+                                  sgn=136, half=128, bd0=128, bd=128, pa0=128, pa=128, pb=128, pd=128, nlt=512, selb=224)),
+                ("int32", dict(pi0=20, pi1=16)),
+                ("float32", dict(nbc=640, gate=320, tt=640, scn=640, mk=16, bia=4, scl=4, cap=4, flip=4, col=8, eight=32, rf=512, yf=2048,
+                                 nbf=512, id32=128, sel0=224, sel=224, dum=32, p5=128))):
     for _n in _l:
         SCRATCH[_n] = ("sbuf", [128, _l[_n]], _dt)
 for _b in range(8):
     SCRATCH["ps%d" % _b] = ("psum", [128, 512], "float32")
 
-SEMAPHORES = (["cv", "cs", "cp", "cg", "ldnb", "ldp0", "ldp1", "ldp2", "ldp3", "sent", "stored", "anb1", "anb2", "anb3", "ard"]
-              + ["apk%d" % _i for _i in range(8)] + ["ay%d" % _i for _i in range(8)])
-
-
-def relay_of(core, topo):
-    return [c for c in topo.cores_of(core) if topo.die(c) != topo.die(core)][0]
-
-
-def relay_program(g, core, owner, T, topo):
-    rank = T.rank_of(owner)
-    n = 0
-    for name, out, in_, plan in (("apk", T.pkl, T.pks, PK), ("ay", T.yl, T.ys, END)):
-        for i, (a, c0, c1, via) in enumerate(plan):
-            if via:
-                to = T.cores[(rank + a) % NR]
-                far = topo.engines(owner, to)
-                g.wait_ge(T.sem[name + str(i)], len([e for e in topo.engines(owner, core) if e not in far]))
-                rid, pid = topo.addr(to, core)
-                g.remote_dma(out[:, 512 * a + c0:512 * a + c1], in_[:, 512 * a + c0:512 * a + c1], T.sem[name + str(i)],
-                             T.sem.sent, pid, rid, topo.mask(core, to))
-                n += len(topo.engines(core, to))
-    if n:
-        g.wait_ge(T.sem.sent, n)
+SEMAPHORES = ["cv", "cs", "cp", "cg", "ldn0", "ldn1", "ldn2", "ldp0", "ldp1", "ldp2", "ldp3", "sent", "stored", "anb1", "anb2", "anb3",
+              "apk1", "apk2", "apk3", "ay1", "ay2", "ay3", "tfl", "tnb", "tpk", "tpay"]
 
 
 def rank_program(g, core, T, topo):
     rank = T.rank_of(core)
     if rank is None:
-        for c in T.cores:
-            if relay_of(c, topo) == core:
-                relay_program(g, core, c, T, topo)
         return
     Q = {"v": g.vector, "s": g.scalar, "p": g.tensor, "g": g, "y": g.sync}
     CS = {"v": "cv", "s": "cs", "p": "cp", "g": "cg"}
@@ -95,267 +82,358 @@ def rank_program(g, core, T, topo):
             wr[w] = [tok]
             rd[w] = []
 
+    def copies(e, pairs, sem, reads, key):
+        deps(e, reads, [key])
+        for out, in_ in pairs:
+            Q[e].dma_start(out, in_).then_inc(T.sem[sem], 16)
+        cnt[sem] = cnt.get(sem, 0) + 16 * len(pairs)
+        wr[key] = [(sem, cnt[sem])]
+
     V, A, PE = g.vector, g.scalar, g.tensor
     ps = [T["ps%d" % b] for b in range(8)]
     peer = [T.cores[(rank + a) % NR] for a in range(NR)]
     dst = [(rank + a) % NR for a in range(NR)]
     src = [(rank - a) % NR for a in range(NR)]
-    relay = relay_of(core, topo)
     far = topo.engines(core, peer[1])
-    near = [e for e in topo.engines(core, relay) if e not in far]
     sent = [0]
 
-    def send(a, out, in_, sem, via, reads, lands):
+    def send(a, out, in_, sem, reads, lands):
         deps("g", reads, [])
-        to, eng = (relay, near) if via else (peer[a], far)
-        rid, pid = topo.addr(to, core)
-        g.remote_dma(in_ if via else out, in_, T.sem[sem], T.sem.sent, pid, rid, sum(1 << e for e in eng))
-        sent[0] += len(eng)
+        rid, pid = topo.addr(peer[a], core)
+        g.remote_dma(out, in_, T.sem[sem], T.sem.sent, pid, rid, topo.mask(core, peer[a]))
+        sent[0] += len(far)
         wr[lands] = [(sem, len(far))]
 
-    def fused(slots, cut, outs, ins, sems, reads):
-        deps("g", reads, [])
-        trs = []
-        for i, a in enumerate(slots):
-            rid, pid = topo.addr(peer[a], core)
-            trs.append(RemoteDMATransfer(dst_ids=[DstId(rid=rid, pnc=pid)], dma_engine_mask=sum(1 << e for e in cut[i]),
-                                         remote_sem=T.sem[sems[i]], src=ins[i], dst=outs[i]))
-            sent[0] += len(cut[i])
-        g.remote_dma_fused(trs, local_sem=T.sem.sent)
-
-    def cuts(n):
-        h, q = len(far) // 2, len(far) // 4
-        return {1: [far], 2: [far[:h], far[h:]], 3: [far[:h], far[h:h + q], far[h + q:]]}[n]
-
-    g.sync.dma_start(T.nbraw[:], T.nb[:]).then_inc(T.sem.ldnb, 16)
-    wr["nbraw"] = [("ldnb", 16)]
-    seen = []
-    for a in [x[0] for x in PK][:2] + [0] + [x[0] for x in PK][2:]:
-        if a in seen:
-            continue
-        seen.append(a)
+    for what, a in LOADS:
         d = dst[a]
+        if what == "n":
+            Q["sy"[a % 2]].dma_start(T.nbq[:, a], T.nb[32 * d:32 * d + 32, :]).then_inc(T.sem["ldn%d" % min(a, 2)], 16)
+            wr[("nbq", min(a, 2))] = [("ldn%d" % min(a, 2), 32 if a > 1 else 16)]
+            continue
         buf = T.pkl if a == 0 else T.pks
         for j in range(4):
             Q["sy"[j % 2]].dma_start(buf[32 * j:32 * j + 32, 512 * a:512 * a + 512],
                                      T.packets[32 * d:32 * d + 32, 512 * j:512 * j + 512]).then_inc(T.sem["ldp%d" % a], 16)
-        wr[("pks", a)] = [("ldp%d" % a, 64)]
+        wr[("pks" if a else "pkl", a)] = [("ldp%d" % a, 64)]
 
-    op("v", lambda: V.memset(T.town[:, 0:2048], M), [], [("to", 0)])
     op("v", lambda: V.memset(T.ones[:], 1.0), [], ["ones"])
-    op("v", lambda: V.memset(T.town[:, 2048:4096], M), [], [("to", 1)])
-    op("s", lambda: A.activation(T.town[:, 4096:6144], T.town[:, 0:2048], ACT.Copy), [("to", 0)], [("to", 2)])
-    op("s", lambda: A.activation(T.town[:, 6144:8192], T.town[:, 0:2048], ACT.Copy), [("to", 0)], [("to", 3)])
-    op("s", [lambda b=b: A.activation(T.ext[:, 512 * b:512 * b + 512], T.ones[:], ACT.Copy, scale=0.0) for b in range(4)],
-       ["ones"], ["ext"])
+    op("g", lambda: g.iota(T.pi0[:], [[-1, 20]], 16, 1), [], ["pi0"])
+    op("v", lambda: V.tensor_scalar(T.pi1[:], T.pi0[:, 0:16], 15, None, ALU.bitwise_and), ["pi0"], ["pi1"])
+    op("v", lambda: V.tensor_scalar(T.col[:, 0:1], T.pi1[:, 0:1], 4.0, M0 - M, ALU.is_lt, ALU.mult), ["pi1"], ["low"])
+    op("v", [lambda b=b: V.tensor_scalar(T.town[:, 512 * b:512 * b + 512], T.ones[:], T.col[:, 0:1], M, ALU.mult, ALU.add)
+             for b in range(4)], ["ones", "low"], [("to", 0)])
+    op("v", [lambda: V.tensor_scalar(T.col[:, 3:4], T.pi1[:, 0:1], -1.0, None, ALU.mult),
+             lambda: V.tensor_scalar(T.mk[:], T.pi1[:], 0.0, None, ALU.is_equal)], ["pi1"], ["mk"])
+    op("v", lambda: V.tensor_copy(T.town[:, 2048:3072], T.town[:, 0:1024]), [("to", 0)], [("to", 1)])
     TO = [("to", b) for b in range(4)]
-    op("g", lambda: g.iota(T.dum[:], [[0, 2], [16, 32]], S + E1, 1), [], ["dum"])
-    op("g", lambda: g.iota(T.pi0[:], [[-1, 4]], 16, 1), [], ["pi0"])
+    op("g", lambda: g.iota(T.dum[:], [[16, 32]], S + E1, 1, allow_small_or_imprecise_dtypes=True), [], ["dum"])
+    op("g", lambda: g.affine_select(T.sel0[:], T.ones[:, 0:224], [[-4, 224]], ALU.is_ge, 0.0, 384, 1), ["ones"], ["sel0"])
+    op("g", lambda: g.affine_select(T.sel[:], T.sel0[:], [[4, 224]], ALU.is_ge, 0.0, -381, -1), ["sel0"], ["sel"])
+    op("s", lambda: A.activation(T.pay0[:, 0:512], T.ones[:], ACT.Copy, scale=0.0), ["ones"], ["pay0"])
+    op("s", lambda: A.activation(T.selb[:], T.sel[:], ACT.Copy), ["sel"], ["selb"])
+    for b in (2, 3):
+        op("s", lambda: A.activation(T.town[:, 2048 * b:2048 * b + 2048], T.town[:, 0:2048], ACT.Copy), [("to", 0)], [("to", b)])
 
-    for a in (1, 2, 3, 0):
-        op("v", [lambda j=j: V.tensor_copy((T.nbs if a else T.nbl)[32 * j:32 * j + 32, a],
-                                           T.nbraw[32 * dst[a]:32 * dst[a] + 32, :, 32 * j:32 * j + 32])
-                 for j in range(4)], ["nbraw"], [("nbs" if a else "nbl", a)])
-    i = 0
-    for x in START:
-        if x[0] == "n":
-            cut = cuts(len(x[1]))
-            fused(x[1], cut, [T.nbl[:, a] for a in x[1]], [T.nbs[:, a] for a in x[1]], ["anb%d" % a for a in x[1]],
-                  [("nbs", a) for a in x[1]])
-            for k, a in enumerate(x[1]):
-                wr[("nbl", a)] = [("anb%d" % a, len(cut[k]))]
+    def summed(a, b):
+        op("v", [lambda: V.tensor_copy(T.nbf[:, 128 * a:128 * b], T.nbq[:, a:b]),
+                 lambda: V.tensor_scalar(T.nlt[:, 128 * a:128 * b], T.nbq[:, a:b], float(S), 32768.0, ALU.is_lt, ALU.mult)],
+           [("nbq", a)], [("nbf", a)])
+        for x in range(a, b):
+            op("p", [lambda j=j, h=h: PE.matmul(ps[x][:, 0:32], (T.sel, T.selb)[h][:, 96 - 32 * j:224 - 32 * j],
+                                                (T.nbf, T.nlt)[h][:, 128 * x + 32 * j:128 * x + 32 * j + 32], j + h == 0, j + h == 4)
+                     for h in range(2) for j in range(4)], [("nbf", a), "sel", "selb"], [("ps", x)])
+        op("v", lambda: V.tensor_copy((T.nbs if a else T.nbl)[:, a:b, 0:128], T.nbq[:, a:b]), [("nbq", a)], [("nbs", a)])
+
+    def single(a):
+        op("v", lambda: V.tensor_tensor(T.p5[:, 32 * a:32 * a + 32], ps[a][:, 0:32], T.dum[:], ALU.min), ["dum"], [("ps", a), ("p5", a)])
+        op("v", lambda: V.tensor_scalar((T.nbs if a else T.nbl)[:, a, 128:160], T.p5[:, 32 * a:32 * a + 32], -float(E1), None, ALU.add),
+           [("p5", a)], [("one", a)])
+
+    def scatter1(a):
+        op("v", lambda: V.tensor_copy(T.town[:, 0:CB].indirect(T.nbl[:, a, 128:160]), T.pkl[:, 512 * a:512 * a + 512]),
+           [("nbl", a) if a else ("one", 0), ("pkl", a)], TO)
+
+    def packets(a):
+        send(a, T.pkl[:, 512 * a:512 * a + 512], T.pks[:, 512 * a:512 * a + 512], "apk%d" % a, [("pks", a)], ("pkl", a))
+
+    def lists(*slots):
+        deps("g", [(x, a) for a in slots for x in ("nbs", "one")], [])
+        n = len(far) // len(slots)
+        trs = []
+        for i, a in enumerate(slots):
+            rid, pid = topo.addr(peer[a], core)
+            trs.append(RemoteDMATransfer(dst_ids=[DstId(rid=rid, pnc=pid)], dma_engine_mask=sum(1 << e for e in far[n * i:n * i + n]),
+                                         remote_sem=T.sem["anb%d" % a], src=T.nbs[:, a], dst=T.nbl[:, a]))
+            wr[("nbl", a)] = [("anb%d" % a, n)]
+        g.remote_dma_fused(trs, local_sem=T.sem.sent)
+        sent[0] += len(far)
+
+    packets(1)
+    summed(1, 2)
+    summed(2, 4)
+    single(1)
+    lists(1)
+    packets(2)
+    summed(0, 1)
+    single(2)
+    single(3)
+    lists(2, 3)
+    packets(3)
+    op("v", lambda: V.tensor_copy(T.town[:, 3072:4096], T.town[:, 0:1024]), [("to", 0)], [("to", 1)])
+    single(0)
+
+    wr[("nbl", 0)] = wr[("nbs", 0)]
+    for what, a in TURNS:
+        if what == "n":
+            copies("y", [(T.nbr[32 * a:32 * a + 32], T.nbl[:, a, 0:128])], "tnb", [("nbl", a)], ("nbr", a))
+            wr["nbr"] = wr[("nbr", a)]
         else:
-            a, c0, c1, via = x[1:]
-            send(a, T.pkl[:, 512 * a + c0:512 * a + c1], T.pks[:, 512 * a + c0:512 * a + c1], "apk%d" % i, via,
-                 [("pks", a)], ("pkl", i))
-            i += 1
-    wr[("pkl", "own")] = wr[("pks", 0)]
-    PKL = {a: [("pkl", i) for i, x in enumerate(PK) if x[0] == a] for a in (1, 2, 3)}
-    PKL[0] = [("pkl", "own")]
+            copies("y", [(T.pkr[32 * a:32 * a + 32, 512 * j:512 * j + 512], T.pkl[32 * j:32 * j + 32, 512 * a:512 * a + 512])
+                         for j in range(4)] if a else [(T.pkr[0:32, :], T.packets[32 * rank:32 * rank + 32, :])],
+                   "tpk", [("pkl", a)], ("pkr", a))
+            wr["pkr"] = wr[("pkr", a)]
 
-    def single(a, b):
-        nb = [("nbl", x) for x in range(a, b)]
-        of = [("offs", x, c) for x in range(a, b) for c in range(0, 32, 8)]
-        op("v", lambda: V.tensor_scalar(T.p1[:, 128 * a:128 * b], T.nbl[:, a:b], E1, None, ALU.add), nb, [("p1", a)])
-        op("v", lambda: V.tensor_scalar(T.p2[:, 128 * a:128 * b], T.p1[:, 128 * a:128 * b], 32767, None, ALU.bitwise_and),
-           [("p1", a)], [("p2", a)])
-        op("v", [lambda x=x: V.tensor_tensor(T.p3[:, 64 * x:64 * x + 64], T.p2[:, 128 * x:128 * x + 64],
-                                             T.p2[:, 128 * x + 64:128 * x + 128], ALU.add) for x in range(a, b)],
-           [("p2", a)], [("p3", a)])
-        op("v", [lambda x=x: V.tensor_tensor(T.p4[:, 32 * x:32 * x + 32], T.p3[:, 64 * x:64 * x + 32],
-                                             T.p3[:, 64 * x + 32:64 * x + 64], ALU.add) for x in range(a, b)],
-           [("p3", a)], [("p4", a)])
-        op("v", lambda: V.tensor_tensor(T.p5[:, 32 * a:32 * b], T.p4[:, 32 * a:32 * b], T.dum[:, 0:32 * (b - a)], ALU.min),
-           [("p4", a), "dum"], [("p5", a)])
-        op("v", lambda: V.tensor_scalar(T.offs[:, 32 * a:32 * b], T.p5[:, 32 * a:32 * b], -float(E1), None, ALU.add), [("p5", a)], of)
+    op("s", [lambda: A.activation(T.col[:, 1:2], T.col[:, 0:1], ACT.Identity, scale=-3.0, bias=-3 * M),
+             lambda: A.activation(T.tt[:, 4:8], T.mk[:, 4:8], ACT.Identity, scale=-24576.0, accum_out=T.col[:, 2:3]),
+             lambda: A.activation(T.tt[:, 0:4], T.mk[:, 0:4], ACT.Identity, scale=X0 - X, bias=X / 4, accum_out=T.col[:, 4:5]),
+             lambda: A.activation(T.cap[:], T.mk[:, 0:4], ACT.Identity, scale=256 - 1e6, bias=1e6),
+             lambda: A.activation(T.bia[:], T.mk[:, 0:4], ACT.Identity, scale=256.0),
+             lambda: A.activation(T.flip[:], T.mk[:, 0:4], ACT.Identity, scale=-2.0, bias=1.0),
+             lambda: A.activation(T.scl[:], T.mk[:, 0:4], ACT.Identity, scale=2.0, bias=-1.0)], ["mk", "low"], ["col", ("t", 0)])
+    scatter1(0)
+    op("v", lambda: V.tensor_scalar(T.pi0[:, 0:1], T.pi0[:, 16:17], 63, None, ALU.bitwise_and), [], ["pi0"])
+    op("v", lambda: V.tensor_scalar(T.col[:, 6:7], T.pi0[:, 0:1], 16.0, 3 * (M - M0), ALU.is_lt, ALU.mult), ["pi0"], ["end0"])
 
-    def scatter1(a, c0, c1, key):
-        op("v", lambda: V.tensor_copy(T.town[:, 0:TW].indirect(T.offs[:, 32 * a + c0 // 16:32 * a + c1 // 16]),
-                                      T.pkl[:, 512 * a + c0:512 * a + c1]),
-           [("offs", a, c) for c in range(0, 32, 8)] + [key], TO)
+    def fill(ap, n, x):
+        return lambda: A.activation(ap, T.ones[:, 0:n], ACT.Copy, scale=x)
 
-    single(0, 1)
-    scatter1(0, 0, 512, ("pkl", "own"))
+    op("s", [fill(T.zz[:, 0:3], 432, 0.0), fill(T.zz[:, 3:6], 432, 0.0)], ["ones"], ["zz"])
+    op("s", [fill(T.tm[:, S:S + 16], 16, 0.0), fill(ps[5][:, 4:160:5], 32, 0.0), fill(ps[6][:, 4:160:5], 32, 0.0),
+             fill(T.nbc[:, 4:640:5], 128, 2 * C), fill(T.half[:], 128, 0.5),
+             lambda: A.activation(T.dig[:, 9], T.ones[:, 0:128], ACT.Identity, scale=T.col[:, 3:4])], ["ones", "mk"],
+       ["tmz", ("ps", 5), ("ps", 6), "nb5", "half", ("dig", 9)])
+
+    def later():
+        op("s", [lambda o=o, n=n: A.activation(T.town[:, CB + o:CB + o + n], T.ones[:, 0:n], ACT.Identity, scale=T.col[:, 2:3])
+                 for o, n in ((0, 512), (512, CAP - 512))] +
+           [fill(T.eight[:], 32, 8.0), fill(T.sgn[:, 0:8], 8, -1.0), lambda: A.activation(T.pd[:], T.ident[:], ACT.Copy, scale=BIG / 2),
+            lambda: A.activation(T.col[:, 5:6], T.col[:, 6:7], ACT.Identity, bias=-3 * M)],
+           ["col", "ident", "end0"], ["left", "eight", "sgn", "pd", "end"])
 
     op("g", lambda: g.affine_select(T.ident[:], T.ones[:, 0:128], [[-1, 128]], ALU.is_equal, 0.0, 0, 1), ["ones"], ["ident"])
-    op("g", lambda: g.affine_select(T.gm0[:], T.ones[:, 0:8], [[-16, 8]], ALU.is_ge, 0.0, 0, 1), ["ones"], ["gm0"])
-    op("g", lambda: g.affine_select(T.gm1[:], T.gm0[:], [[16, 8]], ALU.is_ge, 0.0, 15, -1), ["gm0"], ["gm1"])
     for b in range(4):
         op("g", lambda: g.affine_select(T.wm[32 * b:32 * b + 32, :], T.ones[32 * b:32 * b + 32, 0:128], [[0, 4], [-1, 32]],
                                         ALU.is_equal, 0.0, 0, 1), ["ones"], ["wm"])
-    for b in range(4):
-        op("g", lambda: g.affine_select(T.lfin[32 * b:32 * b + 32, :], T.ones[32 * b:32 * b + 32, :], [[1, 4], [-1, 128]],
-                                        ALU.is_equal, 0.0, 0, 4), ["ones"], ["lfin"])
-    op("v", lambda: V.tensor_scalar(T.pi1[:], T.pi0[:], 15, None, ALU.bitwise_and), ["pi0"], ["pi1"])
-    op("v", [lambda k=k: V.memset(T.wc[:, k:k + 1], WK[k]) for k in range(4)], [], ["wc"])
-    op("v", lambda: V.tensor_scalar(T.mk[:], T.pi1[:], 0.0, None, ALU.is_equal), ["pi1"], ["mk"])
-    op("v", lambda: V.memset(T.gate[:], 0.0), [], ["gate"])
-    op("v", lambda: V.memset(T.tm[:, S:S + 16], 0.0), [], ["tmz"])
-    op("v", lambda: V.tensor_scalar(T.bia[:], T.mk[:], -256.0, None, ALU.mult), ["mk"], ["bia"])
-    op("v", lambda: V.tensor_tensor(T.wp[:], T.mk[:], T.wc[:], ALU.mult), ["mk", "wc"], ["wp"])
-    op("v", lambda: V.tensor_scalar(T.scl[:], T.mk[:], 2.0, -1.0, ALU.mult, ALU.add), ["mk"], ["scl"])
-    op("v", lambda: V.tensor_scalar(T.gate[:, 0:128:4], T.dum[:, 0:32], C - E1, None, ALU.add), ["dum"], ["gate"])
-    op("v", lambda: V.tensor_reduce(T.wcol[:], T.wp[:], AxisListType.X, ALU.add), ["wp"], ["wcol"])
-    op("s", lambda: A.activation(T.bsm[:], T.gm1[:], ACT.Identity, scale=T.wcol[:]), ["gm1", "wcol"], ["bsm"])
-    op("s", [lambda i=i: A.activation(T.ext[:, 129 * i:129 * i + 113:16], T.bsm[:], ACT.Copy) for i in range(16)], ["bsm"], ["ext"])
-    op("s", lambda: A.activation(T.diag[:, 0:128], T.ident[:], ACT.Copy, scale=-1.0), ["ident"], [("diag", 0)])
-    op("s", [lambda k=k: A.activation(T.diag[:, 128 * k:128 * k + 128], T.ident[:], ACT.Identity, scale=T.scl[:, k:k + 1])
-             for k in (1, 2, 3)], ["ident", "scl"], [("diag", 1)])
+    for x0, x1, at, w in ([(0, 1, k, WK[k]) for k in range(5)] + [(1, 5, 4, -1.0), (1, 5, 8, 1.0), (5, 6, 12, -16.0), (5, 6, 13, -1.0)]):
+        z = T.zz[:, x0:x1, 15:128:16]
+        op("g", lambda: g.affine_select(z, z, [[-1, x1 - x0], [-16, 8]], ALU.not_equal, w, -at, 1), [], ["zz"])
+    op("g", [lambda h=h: g.iota(T.gate[:, 160 * h:160 * h + 160], [[16, 32], [-32000, 5]], int(C) + (S, DB)[h], 1,
+                                allow_small_or_imprecise_dtypes=True) for h in range(2)], [], ["gate"])
+    op("g", lambda: g.iota(T.dig[:, 8], [[-1, 128]], 0, 0, allow_small_or_imprecise_dtypes=True), [], [("dig", 8)])
+    op("s", [lambda: A.activation(T.diag[:, 0:128], T.ident[:], ACT.Copy, scale=-1.0),
+             lambda: A.activation(T.id32[:], T.ident[:], ACT.Copy)] +
+       [lambda k=k: A.activation(T.diag[:, 128 * k + 128:128 * k + 256], T.ident[:], ACT.Identity, scale=T.scl[:, k:k + 1])
+        for k in range(4)] + [lambda: A.activation(T.diag[:, 640:768], T.ident[:], ACT.Identity, scale=T.col[:, 4:5]),
+                              lambda: A.activation(T.col[:, 7:8], T.col[:, 4:5], ACT.Identity, bias=-127.5)],
+       ["ident", "col"], ["diag"])
+    op("s", [fill(T.pay0[:, 512 * b:512 * b + 512], 512, 0.0) for b in (1, 2, 3)], ["ones"], ["pay0"])
 
-    single(1, 2)
-    for i, (a, c0, c1, via) in enumerate(PK):
-        if i == 1:
-            single(2, 4)
-            op("v", [lambda k=k: V.tensor_scalar(T.nbc[:, k:512:4], T.nbl[:, :, k, :], C, None, ALU.add) for k in range(4)],
-               [("nbl", x) for x in range(4)], ["nbc"])
-        scatter1(a, c0, c1, ("pkl", i))
+    def digits(b):
+        op("s", [lambda k=k: A.activation(T.dig[:, k], T.nbc[:, k:640:5], ACT.Identity, bias=-64.0, scale=-1.0) for k in range(4)],
+           ["nbc"], [("dig", 0)])
+        op("p", [f for k in range(4) for f in
+                 (lambda k=k: PE.matmul(ps[b][:, 128 * k:128 * k + 128], T.id32[:], T.nbc[:, k:640:5], True, False),
+                  lambda k=k: PE.matmul(ps[b][:, 128 * k:128 * k + 128], T.ident[:], T.dig[:, k], False, True))],
+           ["nbc", ("dig", 0), "ident", "diag"], [("ps", b)])
+
+    def payload(b):
+        op("s", lambda: A.activation(T.dig[:, 4:8], ps[b][:], ACT.Copy), [], [("ps", b), ("dig", 4)])
+        copies("y", [(T.pay0[4 + d:128:16, :], T.dig[:, d]) for d in range(10)], "tpay", [("dig", d) for d in (0, 4, 8, 9)], "pay0")
+        op("g", [lambda r=r: g.affine_select(T.pay[:, r:P:16], T.pay0[:, 128 * r:128 * r + 128], [[0, 128]], ALU.is_ge, 0.0, 0, 0)
+                 for r in range(16)], ["pay0"], ["pay"])
+        for b in range(4):
+            op("g", lambda: g.affine_select(T.lfin[32 * b:32 * b + 32, :], T.ones[32 * b:32 * b + 32, :], [[1, 4], [-1, 128]],
+                                            ALU.is_equal, 0.0, 0, 4), ["ones"], ["lfin"])
+
+    scatter1(1)
+    scatter1(2)
+    scatter1(3)
+    op("g", lambda: g.affine_select(T.bd0[:], T.half[:], [[-16, 8], [0, 16]], ALU.is_ge, 0.0, 0, 1), ["half"], ["bd0"])
+    op("g", lambda: g.affine_select(T.bd[:], T.bd0[:], [[16, 8], [0, 16]], ALU.is_ge, 0.0, 15, -1), ["bd0"], ["bd"])
+    op("g", lambda: g.affine_select(T.pb[:], T.bd[:], [[-1, 128]], ALU.is_ge, 0.0, 0, 1), ["bd"], ["pb"])
+    op("g", lambda: g.affine_select(T.pa0[:], T.bd[:], [[1, 128]], ALU.is_gt, 0.0, 0, -1), ["bd"], ["pa0"])
+    op("g", lambda: g.affine_select(T.pa[:], T.pa0[:], [[-1, 128]], ALU.not_equal, -BIG / 2, 0, 1), ["pa0"], ["pa"])
 
     TM = [("tm", b) for b in range(16)] + ["tmz"]
     bank = [0]
 
-    def merge():
+    def merge(between=(), who="sv" * 8):
         for b in range(16):
-            k = bank[0] % 6
+            k = bank[0] % 5
             bank[0] += 1
             op("p", lambda: PE.matmul(ps[k][:], T.wm[:], T.town[:, 512 * b:512 * b + 512], True, True), TO + ["wm"], [("ps", k)])
-            if b % 2 == 0:
-                op("s", lambda: A.activation(T.tm[:, 512 * b:512 * b + 512], ps[k][:], ACT.Identity, bias=-3 * M),
-                   [], [("ps", k), ("tm", b)])
+            if who[b] == "s":
+                op("s", lambda: A.activation(T.tm[:, 512 * b:512 * b + 512], ps[k][:], ACT.Identity, bias=T.col[:, 1:2]),
+                   ["col"], [("ps", k), ("tm", b)])
             else:
-                op("v", lambda: V.tensor_scalar(T.tm[:, 512 * b:512 * b + 512], ps[k][:], -3 * M, None, ALU.add),
-                   [], [("ps", k), ("tm", b)])
+                op("v", lambda: V.tensor_scalar(T.tm[:, 512 * b:512 * b + 512], ps[k][:], T.col[:, 1:2], None, ALU.add),
+                   ["col"], [("ps", k), ("tm", b)])
+            if b in between:
+                between[b]()
 
-    def flags(t, half):
-        fns = []
-        for a in (2 * half, 2 * half + 1):
-            d = dst[a]
-            for c in range(16):
-                o = 128 * t + 32 * a + c
-                fns.append(lambda o=o, d=d, c=c: PE.matmul(ps[7][:, o:o + 17:16], T.tm[:, P * d + c:P * d + P:16],
-                                                           T.ident[:, 0:17:16], True, True))
-        op("p", fns, TM + ["ident"], [("ps", 7)])
+    def flags(t):
+        copies("y", [(T.fl[32 * a:32 * a + 32, 128 * t:128 * t + 128], T.tm[0:32:16, P * dst[a]:P * dst[a] + P]) for a in range(NR)],
+               "tfl", TM, "fl")
+        for b in TM:
+            rd[b] = rd.get(b, []) + wr["fl"]
+
+    def unwrap(k, o, x):
+        op("p", [lambda r=r: PE.matmul(ps[k][:, o:o + 48], T.zz[:, x, 15 - r:143 - r], T.town[:, CB + r:DB:16], r == 0, r == 15)
+                 for r in range(16)], ["left", "zz"], [("ps", k)])
+
+    def numbers():
+        op("v", lambda: V.tensor_copy(T.nb4[:, 4], ps[5][:, 320:368]), [], [("ps", 5), ("nb4", 4)])
+        op("s", lambda: A.activation(T.pk4[:], T.pkr[:].indirect(T.nb4[:, 4]), ACT.Copy), ["pkr", ("nb4", 4)], ["pk4"])
+
+    def places(h):
+        op("v", lambda: V.tensor_scalar(T.nb4[:, 2 * h:2 * h + 2], ps[6 - h][:, 368:464], -C, None, ALU.add), [],
+           [("ps", 6 - h), ("nb4", 2 * h), ("nb4", 2 * h + 1)])
 
     def peel(t):
-        n = len(CHUNKS)
+        chunks, order = ROUND[t]
+        steps = [(x[0], int(x[1])) for x in order.split()]
+        ends = [i for c, i in steps if c == "d"]
         win = T.tm[:, 0:S + 1]
-
-        def span(i):
-            a, c0, c1 = CHUNKS[i]
-            return a, c0, c1, 512 * a + 16 * c0, 16 * (c1 - c0)
-
-        def keys(name, i):
-            a, c0, c1 = CHUNKS[i]
-            return [(name, a, c) for c in range(c0, c1, 8)]
-
-        def gath(i, k):
-            a, c0, c1, u, w = span(i)
-            out = T.gat[:, P * k + u:P * k + u + w]
-            ind = win.indirect(T.nbl[:, a, k, c0:c1])
-            if k == 0:
-                op("v", lambda: V.tensor_copy(out, ind), TM + [("nbl", a)], keys(("g", k), i))
-            else:
-                op("s", lambda: A.activation(out, ind, ACT.Abs, bias=T.bia[:, k:k + 1]), TM + [("nbl", a), "bia"], keys(("g", k), i))
-
-        def gx(i, k):
-            if i == n:
-                return
-            gath(i, k)
-            a, c0, c1, u, w = span(i)
-            x = ps[i % 3][:, 0:w]
-            if k == 1:
-                op("p", lambda: PE.matmul(x, T.ident[:], T.pkl[:, u:u + w], True, False), PKL[a] + ["ident"], [("ps", i % 3)])
-            for kk in ((k,) if k != 2 else (0, 2)):
-                op("p", lambda: PE.matmul(x, T.diag[:, 128 * kk:128 * kk + 128], T.gat[:, P * kk + u:P * kk + u + w], False,
-                                          kk == 3 and i not in RS),
-                   keys(("g", kk), i) + [("diag", 0), ("diag", 1)], [("ps", i % 3)])
-
-        def quot(i):
-            a, c0, c1, u, w = span(i)
-            op("s", lambda: A.activation(T.qq[:, u:u + w], ps[i % 3][:, 0:w], ACT.Identity, bias=-127.5),
-               [], [("ps", i % 3)] + keys("q", i))
-            f = ps[3 + i % 2][:, 0:c1 - c0]
-            op("p", [lambda r=r: PE.matmul(f, T.ext[:, 128 * r:128 * r + 128], T.qq[:, u + r:u + w:16], r == 0, r == 15)
-                     for r in range(16)], keys("q", i) + ["ext"], [("ps", 3 + i % 2)])
-            if i in RS:
-                op("p", lambda: PE.matmul(ps[i % 3][:, 0:w], T.diag[:, 0:128], T.qq[:, u:u + w], False, True),
-                   keys("q", i), [("ps", i % 3)])
-
-        def dist(i):
-            a, c0, c1, u, w = span(i)
-            m = c1 - c0
-            op("s", [lambda k=k: A.activation(ps[5 + i % 2][:, k:4 * m:4], ps[3 + i % 2][:, 0:m], ACT.Abs, bias=-LAM[k] * M)
-                     for k in range(4)], [], [("ps", 3 + i % 2), ("ps", 5 + i % 2)])
-            if i in RS:
-                op("s", lambda: A.activation(T.rr[:, u:u + w], ps[i % 3][:, 0:w], ACT.Copy), [], [("ps", i % 3)] + keys("r", i))
-
-        def release(i):
-            a, c0, c1, u, w = span(i)
-            m = c1 - c0
-            o = 128 * a + 4 * c0
-            if i not in RS:
-                op("v", lambda: V.tensor_tensor(T.rr[:, u:u + w], ps[i % 3][:, 0:w], T.qq[:, u:u + w], ALU.subtract),
-                   keys("q", i), [("ps", i % 3)] + keys("r", i))
-            op("v", lambda: V.tensor_tensor(T.tt[:, o:o + 4 * m], ps[5 + i % 2][:, 0:4 * m], T.nbc[:, o:o + 4 * m], ALU.max),
-               ["nbc"], [("ps", 5 + i % 2)] + keys("t", i))
-            op("v", lambda: V.tensor_tensor_scan(T.scn[:, o:o + 4 * m], T.gate[:, 0:4 * m], T.tt[:, o:o + 4 * m], 0.0, ALU.max, ALU.min),
-               keys("t", i) + ["gate"], keys("sc", i))
-            of = T.offs[:, 32 * a + c0:32 * a + c1]
-            op("v", lambda: V.tensor_scalar(of, T.scn[:, o + 3:o + 4 * m:4], -C, None, ALU.add), keys("sc", i), keys("offs", i))
-            op("v", lambda: V.tensor_copy(T.town[:, 0:TW].indirect(of), T.rr[:, u:u + w]), keys("offs", i) + keys("r", i), TO)
-
-        flags(t - 2, 0)
-        for i in range(n):
-            gath(i, 0)
-        for k in (1, 2, 3):
-            gx(0, k)
-        for i in range(n):
-            for c in ORDER:
-                if c == "q":
-                    quot(i)
-                elif c == "d":
-                    dist(i)
+        pk = T.pk4 if t == 4 else T.pkr
+        held = {i: [] for i in range(len(chunks))}
+        done = {i: [] for i in range(len(chunks))}
+        free, xb, zb = [0, 1, 2, 3], {}, {}
+        flags(t - 2)
+        for c, i in steps:
+            if c in "oune":
+                if c == "o":
+                    rounds_out(i)
+                elif c == "e":
+                    (lambda: digits(7), lambda: payload(7), later)[i]()
+                elif t == 2:
+                    op("v", [lambda k=k: V.tensor_scalar(T.nbc[:, k:640:5], T.nbr[:, k], C, None, ALU.add) for k in range(4)], ["nbr"], ["nbc"])
+                elif c == "u":
+                    places(1)
                 else:
-                    gx(i + 1, int(c))
-            release(i)
-            if i == FL2:
-                flags(t - 2, 1)
-            if t == 4 and i == FL2 + 1:
-                rounds_out()
+                    op("s", [lambda k=k: A.activation(T.nbc[:, k:240:5], ps[6 - k // 2][:, 368 + 48 * (k % 2):416 + 48 * (k % 2)], ACT.Copy)
+                             for k in range(4)] + [fill(T.nbc[:, 4:240:5], 48, 2 * C)], [], [("ps", 5), ("ps", 6), "nbc", "nb5"])
+                continue
+            h = min(n for n, e in enumerate(ends) if e >= i)
+            b0 = chunks[ends[h - 1]][1] if h else 0
+            c0, c1 = (b0, chunks[i][1]) if c in "dpabcs" else chunks[i]
+            u, w, m, o, e = 16 * c0, 16 * (c1 - c0), c1 - c0, 5 * c0, 5 * c1
+            h %= 2
+            f, st, dd = ps[4][:, 64 * h + c0 - b0:64 * h + c1 - b0], ps[4][:, 128 + 64 * h:128 + 64 * h + m], ps[5 + h]
+            F, D = ("ps", 4), ("ps", 5 + h)
+            if i not in xb and (c in "0123" or len(held[i]) == 3):
+                xb[i] = free.pop(0)
+            if i in xb and c not in "dpabcs":
+                x, B = ps[xb[i]][:, 0:w], ("ps", xb[i])
 
-    def rounds_out():
-        op("s", lambda: A.activation(T.sg[:], ps[7][:, 0:384], ACT.Sign, bias=-1000.0), [], [("ps", 7), "sg"])
-        op("p", [lambda t=t: PE.matmul(ps[7][:, 384:512], T.ident[:], T.sg[:, 128 * t:128 * t + 128], t == 0, t == 2)
-                 for t in range(3)], ["sg", "ident"], [("ps", 7)])
-        op("s", lambda: A.activation(T.rs[:], ps[7][:, 384:512], ACT.Identity, bias=2.5, scale=0.5), [], [("ps", 7), "rs"])
-        fused((1, 2, 3), cuts(3), [T.rl[:, 32 * a:32 * a + 32] for a in (1, 2, 3)], [T.rs[:, 32 * a:32 * a + 32] for a in (1, 2, 3)],
-              ["ard"] * 3, ["rs"])
-        wr["rl"] = [("ard", len(far))]
+            def keys(name):
+                return [(name, cc) for cc in range(c0, c1, 4)]
+
+            def place(k, last):
+                sign = 0 if ("vwxy"[k], i) in steps else k + 1
+                return lambda: PE.matmul(x, T.diag[:, 128 * sign:128 * sign + 128], T.gat[:, P * k + u:P * k + u + w], False, last)
+
+            def first(lift):
+                return ([lambda: PE.matmul(x, T.ident[:], pk[:, u:u + w], True, False)] +
+                        [lambda: PE.matmul(x, T.diag[:, 640:768], T.ones[:, 0:w], False, False)] * lift)
+
+            def less():
+                done[i].append(c)
+                if len(done[i]) == 6:
+                    xb[i] = zb[i]
+                    op("p", lambda: PE.matmul(ps[xb[i]][:, 0:w], T.diag[:, 0:128], T.qq[:, u:u + w], False, True), keys("q"), [("ps", xb[i])])
+
+            if c in "vwxy0123":
+                k = "vwxy0123".index(c) % 4
+                out = T.gat[:, P * k + u:P * k + u + w]
+                lst, key = (T.nb4[:, k, c0:c1], ("nb4", k)) if t == 4 else (T.nbr[:, k, c0:c1], "nbr")
+                if c in "vwxy":
+                    op("v", lambda: V.tensor_scalar(out, win.indirect(lst), T.cap[:, k:k + 1], None, ALU.min), TM + [key, "col"], keys(("g", k)))
+                else:
+                    op("s", lambda: A.activation(out, win.indirect(lst), ACT.Relu, bias=T.bia[:, k:k + 1], scale=T.flip[:, k:k + 1]),
+                       TM + [key, "col"], keys(("g", k)))
+                held[i].append(k)
+                if c not in "vwxy" or len(done[i] + held[i]) == 4:
+                    if not done[i]:
+                        op("p", first(("z", i) not in steps), ["pk4" if t == 4 else "pkr", "ident", "diag"], [B])
+                    for kk in held[i]:
+                        done[i].append(kk)
+                        op("p", place(kk, len(done[i]) == 4), keys(("g", kk)) + ["diag"], [B])
+                    held[i] = []
+            elif c in "qQ":
+                bias = T.col[:, 7:8] if ("z", i) in steps else -127.5
+                if c == "q":
+                    op("s", lambda: A.activation(T.qq[:, u:u + w], x, ACT.Relu, bias=bias), ["diag"], [B] + keys("q"))
+                else:
+                    op("v", lambda: V.tensor_scalar(T.qq[:, u:u + w], x, bias, 0.0, ALU.add, ALU.max), ["diag"], [B] + keys("q"))
+                op("p", [lambda r=r: PE.matmul(f, T.zz[:, 0, 15 - r:143 - r], T.qq[:, u + r:u + w:16], r == 0, r == 15)
+                         for r in range(16)], keys("q") + ["zz"], [F])
+                if ("z", i) in steps:
+                    free.append(xb[i])
+                    less()
+            elif c == "d":
+                if t == 3:
+                    op("s", lambda: A.activation(T.sgn[:, 8 + c0:8 + c1], f, ACT.Sign, bias=TWO, scale=-1.0), [], [F, "sgn"])
+                op("s", [lambda k=k: A.activation(dd[:, k:5 * m:5], f, ACT.Abs, bias=-LAM[k]) for k in range(4)], [], [F, D])
+                if t == 3:
+                    op("p", [lambda: PE.matmul(st, T.pa[:], T.sgn[:, 8 + c0:8 + c1], True, False),
+                             lambda: PE.matmul(st, T.pb[:], T.sgn[:, 7 + c0:7 + c1], False, False),
+                             lambda: PE.matmul(st, T.pd[:], T.sgn[:, 7 + c0:7 + c1], False, True)],
+                       ["sgn", "pa", "pb", "pd"], [F])
+            elif c == "z":
+                zb[i] = free.pop(0)
+                x, B = ps[zb[i]][:, 0:w], ("ps", zb[i])
+                op("p", first(True) + [place(kk, False) for kk in range(4)], [y for kk in range(4) for y in keys(("g", kk))], [B])
+                less()
+            elif c == "r":
+                if i not in zb:
+                    op("v", lambda: V.tensor_tensor(x if t == 3 else T.rr[:, u:u + w], x, T.qq[:, u:u + w], ALU.subtract),
+                       keys("q"), [B] + keys("r"))
+                if t == 3:
+                    op("v", lambda: V.tensor_tensor(T.rr[:, u:u + w], x, T.pay[:, u:u + w], ALU.max), ["pay"], [B] + keys("r"))
+                elif i in zb:
+                    op("s", lambda: A.activation(T.rr[:, u:u + w], x, ACT.Copy), [], [B] + keys("r"))
+                free.append(xb[i])
+            elif c == "s":
+                op("v", lambda: V.tensor_copy(T.town[:, 0:TW if t == 3 else CB].indirect(T.offs[:, c0:c1]), T.rr[:, u:u + w]),
+                   keys("offs") + keys("r"), TO + ["left"] * (t == 3))
+            elif c == "p":
+                op("v", lambda: V.tensor_tensor_scan(T.nbc[:, o + 4:e:5], st, T.eight[:, 0:m],
+                                                     T.nbc[:, o - 1:o] if c0 else C + CB + BIG, ALU.add, ALU.add),
+                   ["eight"], [F, "nb5"])
+            elif c == "a":
+                op("v", lambda: V.tensor_tensor(T.tt[:, o:e], dd[:, 0:5 * m], T.nbc[:, o:e], ALU.max), ["nbc", "nb5"], [D] + keys("t"))
+            elif c == "b":
+                op("v", lambda: V.tensor_tensor_scan(T.scn[:, o:e], T.gate[:, 160 * (t == 3):160 * (t == 3) + 5 * m], T.tt[:, o:e], 0.0, ALU.max, ALU.min),
+                   keys("t") + ["gate"], keys("sc"))
+            else:
+                op("v", lambda: V.tensor_scalar(T.offs[:, c0:c1], T.scn[:, o + 4:e:5], -C, None, ALU.add), keys("sc"), keys("offs"))
+
+    def rounds_out(half):
+        if half == 0:
+            op("s", lambda: A.activation(T.sg[:], T.fl[:], ACT.Sign, bias=-1000.0), ["fl"], ["sg"])
+            op("p", [lambda t=t: PE.matmul(ps[7][:, 384:512], T.sg[:, 128 * t:128 * t + 128], T.ident[:], t == 0, t == 2)
+                     for t in range(3)], ["sg", "ident"], [("ps", 7)])
+        else:
+            op("s", lambda: A.activation(T.ys[:, :, 512:544], ps[7][:, 384:512], ACT.Identity, bias=2.5, scale=0.5), [], [("ps", 7), "rs"])
 
     merge()
     peel(2)
     merge()
     peel(3)
-    merge()
+    merge(dict(zip(LAST[0], (lambda: unwrap(5, 320, 5), numbers, lambda: unwrap(6, 368, 1), lambda: unwrap(6, 416, 2), lambda: places(0)))),
+          LAST[1])
+    unwrap(5, 368, 3)
+    unwrap(5, 416, 4)
     peel(4)
 
     stored = [0]
@@ -365,32 +443,35 @@ def rank_program(g, core, T, topo):
         Q[e].dma_start(out, in_).then_inc(T.sem.stored, 16)
         stored[0] += 16
 
-    for a in range(4):
+    def rounds_in(a):
+        op("p", lambda: PE.matmul(ps[4 + a][0:32, 0:128], (T.yl if a else T.ys)[:, a, 512:544], T.ident[:], True, True),
+           [("yl", a) if a else "rs"], [("ps", 4 + a)])
+        op("v", lambda: V.tensor_copy(T.rf[0:32, 128 * a:128 * a + 128], ps[4 + a][0:32, 0:128]), [], [("ps", 4 + a), ("rf", a)])
+        store("s", T.rounds[2 * src[a]:2 * src[a] + 2, :], T.rf[0:32, 128 * a:128 * a + 128], [("rf", a)])
+
+    for i, a in enumerate((1, 2, 3, 0)):
+        o = P * dst[a]
         for h in range(2):
-            buf = T.rs if a == 0 else T.rl
-            store("y", T.rounds[2 * src[a] + h], buf[:, 32 * a + 16 * h:32 * a + 16 * h + 16], ["rs" if a == 0 else "rl"])
-    for i, (a, c0, c1, via) in enumerate(list(END) + [(0, 0, 512, False)]):
-        k = i % 6
-        w = c1 - c0
-        o = P * dst[a] + 4 * c0
-        op("p", [lambda j=j: PE.matmul(ps[k][:, 0:w], T.lfin[:, 128 * j:128 * j + 128], T.town[:, o + w * j:o + w * j + w],
-                                       j == 0, j == 3) for j in range(4)], TO + ["lfin"], [("ps", k)])
-        out = T.yf[:, 0:512] if a == 0 else T.ys[:, 512 * a + c0:512 * a + c1]
-        if i % 2 == 0:
-            op("v", lambda: V.tensor_scalar(out, ps[k][:, 0:w], -3 * M, None, ALU.add), [], [("ps", k), ("ys", i)])
-        else:
-            op("s", lambda: A.activation(out, ps[k][:, 0:w], ACT.Identity, bias=-3 * M), [], [("ps", k), ("ys", i)])
+            k, u = (2 * i + h) % 4, 256 * h
+            op("p", [lambda j=j: PE.matmul(ps[k][:, 0:256], T.lfin[:, 128 * j:128 * j + 128], T.town[:, o + 512 * j + u:o + 512 * j + u + 256],
+                                           j == 0, j == 3) for j in range(4)], TO + ["lfin"], [("ps", k)])
+            out = T.ys[:, a, u:u + 256] if a else T.yf[:, u:u + 256]
+            if h:
+                op("v", lambda: V.tensor_scalar(out, ps[k][:, 0:256], T.col[:, 5:6], None, ALU.add), ["end"], [("ps", k), ("ys", a, h)])
+            else:
+                op("s", lambda: A.activation(out, ps[k][:, 0:256], ACT.Identity, bias=T.col[:, 5:6]), ["end"], [("ps", k), ("ys", a, h)])
         if a:
-            send(a, T.yl[:, 512 * a + c0:512 * a + c1], out, "ay%d" % i, via, [("ys", i)], ("yl", i))
+            send(a, T.yl[:, a], T.ys[:, a], "ay%d" % a, [("ys", a, 0), ("ys", a, 1), "rs"], ("yl", a))
         else:
-            store("s", T.y[32 * rank:32 * rank + 32, :], out, [("ys", i)])
-    for i, (a, c0, c1, via) in sorted(enumerate(END), key=lambda x: x[1][3]):
-        o = 512 * a + c0
-        h = (c1 - c0) // 2
-        op("v", lambda: V.tensor_copy(T.yf[:, o:o + h], T.yl[:, o:o + h]), [("yl", i)], [("yf", i, 0)])
-        op("s", lambda: A.activation(T.yf[:, o + h:o + 2 * h], T.yl[:, o + h:o + 2 * h], ACT.Copy), [("yl", i)], [("yf", i, 1)])
-        store("y", T.y[32 * src[a]:32 * src[a] + 32, 4 * c0:4 * c1], T.yf[:, o:o + 2 * h], [("yf", i, 0), ("yf", i, 1)])
+            store("y", T.y[32 * rank:32 * rank + 32, :], T.yf[:, 0:512], [("ys", a, 0), ("ys", a, 1)])
+    rounds_in(0)
+    for a in (1, 2, 3):
+        o = 512 * a
+        op("v", lambda: V.tensor_copy(T.yf[:, o:o + 256], T.yl[:, a, 0:256]), [("yl", a)], [("yf", a, 0)])
+        op("s", lambda: A.activation(T.yf[:, o + 256:o + 512], T.yl[:, a, 256:512], ACT.Copy), [("yl", a)], [("yf", a, 1)])
+        store("y", T.y[32 * src[a]:32 * src[a] + 32, :], T.yf[:, o:o + 512], [("yf", a, 0), ("yf", a, 1)])
+        rounds_in(a)
     g.sync.wait_ge(T.sem.stored, stored[0])
     g.wait_ge(T.sem.sent, sent[0])
-    for e in cnt:
+    for e in CS:
         wait("g", (CS[e], cnt[e]))

from concourse.bass import DstId, RemoteDMATransfer
from concourse.mybir import AluOpType as ALU, ActivationFunctionType as ACT

S, P, NR, CAP = 8192, 2048, 4, 768
M, M0 = 61440.0, 24576.0
X, X0 = 96256.0, 61440.0
C = 16384.0
E1 = 3 * S + 32768
CB = S + 640
DB = CB + CAP
TW = DB + 640
BIG = 2048.0
WK = (-3.0, -1.0, 1.0, 3.0, 7.0)
LAM = [7 * (X - M - 384) + w * M0 for w in WK[:4]]
TWO = 134000.0
FULL = ((0, 32), (32, 64), (64, 96), (96, 128))
ROUND = {
    2: (FULL, "n0 11 30 w0 20 v0 w2 e0 01 x1 y3 q0 y2 y1 r0 22 e1 d0 a0 Q1 02 13 03 d1 q2 b0 c0 r1 s0 a1 r2 23 b1 d2 q3 c1 a2 z3 s1 d3 b2 a3 c2 b3 s2 r3 c3 e2 s3"),
    3: (FULL, "x0 30 v0 x1 10 11 y1 q0 v1 22 v2 r0 d0 p0 a0 z1 q1 b0 12 32 33 d1 z2 c0 s0 p1 q2 23 r1 a1 b1 c1 s1 13 03 r2 d2 p2 q3 a2 z3 b2 c2 d3 s2 p3 a3 r3 b3 c3 s3"),
    4: (((0, 28), (28, 48)), "u0 10 v0 30 x0 x1 01 w1 q0 y1 z1 n0 r0 d0 q1 a0 d1 b0 r1 c0 s0 a1 b1 o0 c1 o1 s1"),
}
LAST = ((3, 8, 10, 14, 15), "svsvsvsvsvvvsvsv")
TURNS = (("n", 0), ("n", 1), ("p", 0), ("p", 1), ("n", 2), ("n", 3), ("p", 2), ("p", 3))
LOADS = (("p", 1), ("n", 1), ("n", 2), ("n", 3), ("n", 0), ("p", 2), ("p", 0), ("p", 3))

SCRATCH = {"ys": ("sbuf", [128, 4, 544], "bfloat16"), "yl": ("sbuf", [128, 4, 544], "bfloat16"),
           "nbq": ("sbuf", [128, 4, 128], "int32"), "nbs": ("sbuf", [128, 4, 160], "uint16"),
           "nbl": ("sbuf", [128, 4, 160], "uint16"), "nbr": ("sbuf", [128, 4, 128], "uint16"),
           "nb4": ("sbuf", [128, 5, 48], "uint16"), "offs": ("sbuf", [128, 128], "uint16"),
           "dig": ("sbuf", [128, 10, 128], "bfloat16"), "zz": ("sbuf", [128, 6, 144], "bfloat16")}
for _dt, _l in (("bfloat16", dict(pks=2048, pkl=2048, pkr=2048, pk4=CAP, town=TW, tm=S + 16, gat=8192, qq=2048, rr=2048, ones=512,
                                  ident=128, diag=768, wm=128, lfin=512, sg=384, fl=384, pay0=2048, pay=2048,
                                  sgn=136, half=128, bd0=128, bd=128, pa0=128, pa=128, pb=128, pd=128, nlt=512, selb=224)),
                ("int32", dict(pi0=20, pi1=16)),
                ("float32", dict(nbc=640, gate=320, tt=640, scn=640, mk=16, bia=4, scl=4, cap=4, flip=4, col=8, eight=32, rf=512, yf=2048,
                                 nbf=512, id32=128, sel0=224, sel=224, dum=32, p5=128))):
    for _n in _l:
        SCRATCH[_n] = ("sbuf", [128, _l[_n]], _dt)
for _b in range(8):
    SCRATCH["ps%d" % _b] = ("psum", [128, 512], "float32")

SEMAPHORES = ["cv", "cs", "cp", "cg", "ldn0", "ldn1", "ldn2", "ldp0", "ldp1", "ldp2", "ldp3", "sent", "stored", "anb1", "anb2", "anb3",
              "apk1", "apk2", "apk3", "ay1", "ay2", "ay3", "tfl", "tnb", "tpk", "tpay"]


def rank_program(g, core, T, topo):
    rank = T.rank_of(core)
    if rank is None:
        return
    Q = {"v": g.vector, "s": g.scalar, "p": g.tensor, "g": g, "y": g.sync}
    CS = {"v": "cv", "s": "cs", "p": "cp", "g": "cg"}
    cnt = {"v": 0, "s": 0, "p": 0, "g": 0}
    waited = {e: {} for e in Q}
    wr, rd = {}, {}

    def wait(e, tok):
        if waited[e].get(tok[0], 0) < tok[1]:
            Q[e].wait_ge(T.sem[tok[0]], tok[1])
            waited[e][tok[0]] = tok[1]

    def deps(e, reads, writes):
        need = {}
        for t in [t for r in reads for t in wr.get(r, [])] + [t for w in writes for t in wr.get(w, []) + rd.get(w, [])]:
            need[t[0]] = max(need.get(t[0], 0), t[1])
        for s in need:
            if not (e == "p" and s == "cp"):
                wait(e, (s, need[s]))

    def op(e, fns, reads, writes):
        if e == "g":
            writes = writes + ["pool"]
        deps(e, reads, writes)
        ins = None
        for f in (fns if isinstance(fns, list) else [fns]):
            ins = f()
        cnt[e] += 1
        ins.then_inc(T.sem[CS[e]], 1)
        tok = (CS[e], cnt[e])
        for r in reads:
            rd[r] = [t for t in rd.get(r, []) if t[0] != tok[0]] + [tok]
        for w in writes:
            wr[w] = [tok]
            rd[w] = []

    def copies(e, pairs, sem, reads, key):
        deps(e, reads, [key])
        for out, in_ in pairs:
            Q[e].dma_start(out, in_).then_inc(T.sem[sem], 16)
        cnt[sem] = cnt.get(sem, 0) + 16 * len(pairs)
        wr[key] = [(sem, cnt[sem])]

    V, A, PE = g.vector, g.scalar, g.tensor
    ps = [T["ps%d" % b] for b in range(8)]
    peer = [T.cores[(rank + a) % NR] for a in range(NR)]
    dst = [(rank + a) % NR for a in range(NR)]
    src = [(rank - a) % NR for a in range(NR)]
    far = topo.engines(core, peer[1])
    sent = [0]

    def send(a, out, in_, sem, reads, lands):
        deps("g", reads, [])
        rid, pid = topo.addr(peer[a], core)
        g.remote_dma(out, in_, T.sem[sem], T.sem.sent, pid, rid, topo.mask(core, peer[a]))
        sent[0] += len(far)
        wr[lands] = [(sem, len(far))]

    for what, a in LOADS:
        d = dst[a]
        if what == "n":
            Q["sy"[a % 2]].dma_start(T.nbq[:, a], T.nb[32 * d:32 * d + 32, :]).then_inc(T.sem["ldn%d" % min(a, 2)], 16)
            wr[("nbq", min(a, 2))] = [("ldn%d" % min(a, 2), 32 if a > 1 else 16)]
            continue
        buf = T.pkl if a == 0 else T.pks
        for j in range(4):
            Q["sy"[j % 2]].dma_start(buf[32 * j:32 * j + 32, 512 * a:512 * a + 512],
                                     T.packets[32 * d:32 * d + 32, 512 * j:512 * j + 512]).then_inc(T.sem["ldp%d" % a], 16)
        wr[("pks" if a else "pkl", a)] = [("ldp%d" % a, 64)]

    op("v", lambda: V.memset(T.ones[:], 1.0), [], ["ones"])
    op("g", lambda: g.iota(T.pi0[:], [[-1, 20]], 16, 1), [], ["pi0"])
    op("v", lambda: V.tensor_scalar(T.pi1[:], T.pi0[:, 0:16], 15, None, ALU.bitwise_and), ["pi0"], ["pi1"])
    op("v", lambda: V.tensor_scalar(T.col[:, 0:1], T.pi1[:, 0:1], 4.0, M0 - M, ALU.is_lt, ALU.mult), ["pi1"], ["low"])
    op("v", [lambda b=b: V.tensor_scalar(T.town[:, 512 * b:512 * b + 512], T.ones[:], T.col[:, 0:1], M, ALU.mult, ALU.add)
             for b in range(4)], ["ones", "low"], [("to", 0)])
    op("v", [lambda: V.tensor_scalar(T.col[:, 3:4], T.pi1[:, 0:1], -1.0, None, ALU.mult),
             lambda: V.tensor_scalar(T.mk[:], T.pi1[:], 0.0, None, ALU.is_equal)], ["pi1"], ["mk"])
    op("v", lambda: V.tensor_copy(T.town[:, 2048:3072], T.town[:, 0:1024]), [("to", 0)], [("to", 1)])
    TO = [("to", b) for b in range(4)]
    op("g", lambda: g.iota(T.dum[:], [[16, 32]], S + E1, 1, allow_small_or_imprecise_dtypes=True), [], ["dum"])
    op("g", lambda: g.affine_select(T.sel0[:], T.ones[:, 0:224], [[-4, 224]], ALU.is_ge, 0.0, 384, 1), ["ones"], ["sel0"])
    op("g", lambda: g.affine_select(T.sel[:], T.sel0[:], [[4, 224]], ALU.is_ge, 0.0, -381, -1), ["sel0"], ["sel"])
    op("s", lambda: A.activation(T.pay0[:, 0:512], T.ones[:], ACT.Copy, scale=0.0), ["ones"], ["pay0"])
    op("s", lambda: A.activation(T.selb[:], T.sel[:], ACT.Copy), ["sel"], ["selb"])
    for b in (2, 3):
        op("s", lambda: A.activation(T.town[:, 2048 * b:2048 * b + 2048], T.town[:, 0:2048], ACT.Copy), [("to", 0)], [("to", b)])

    def summed(a, b):
        op("v", [lambda: V.tensor_copy(T.nbf[:, 128 * a:128 * b], T.nbq[:, a:b]),
                 lambda: V.tensor_scalar(T.nlt[:, 128 * a:128 * b], T.nbq[:, a:b], float(S), 32768.0, ALU.is_lt, ALU.mult)],
           [("nbq", a)], [("nbf", a)])
        for x in range(a, b):
            op("p", [lambda j=j, h=h: PE.matmul(ps[x][:, 0:32], (T.sel, T.selb)[h][:, 96 - 32 * j:224 - 32 * j],
                                                (T.nbf, T.nlt)[h][:, 128 * x + 32 * j:128 * x + 32 * j + 32], j + h == 0, j + h == 4)
                     for h in range(2) for j in range(4)], [("nbf", a), "sel", "selb"], [("ps", x)])
        op("v", lambda: V.tensor_copy((T.nbs if a else T.nbl)[:, a:b, 0:128], T.nbq[:, a:b]), [("nbq", a)], [("nbs", a)])

    def single(a):
        op("v", lambda: V.tensor_tensor(T.p5[:, 32 * a:32 * a + 32], ps[a][:, 0:32], T.dum[:], ALU.min), ["dum"], [("ps", a), ("p5", a)])
        op("v", lambda: V.tensor_scalar((T.nbs if a else T.nbl)[:, a, 128:160], T.p5[:, 32 * a:32 * a + 32], -float(E1), None, ALU.add),
           [("p5", a)], [("one", a)])

    def scatter1(a):
        op("v", lambda: V.tensor_copy(T.town[:, 0:CB].indirect(T.nbl[:, a, 128:160]), T.pkl[:, 512 * a:512 * a + 512]),
           [("nbl", a) if a else ("one", 0), ("pkl", a)], TO)

    def packets(a):
        send(a, T.pkl[:, 512 * a:512 * a + 512], T.pks[:, 512 * a:512 * a + 512], "apk%d" % a, [("pks", a)], ("pkl", a))

    def lists(*slots):
        deps("g", [(x, a) for a in slots for x in ("nbs", "one")], [])
        n = len(far) // len(slots)
        trs = []
        for i, a in enumerate(slots):
            rid, pid = topo.addr(peer[a], core)
            trs.append(RemoteDMATransfer(dst_ids=[DstId(rid=rid, pnc=pid)], dma_engine_mask=sum(1 << e for e in far[n * i:n * i + n]),
                                         remote_sem=T.sem["anb%d" % a], src=T.nbs[:, a], dst=T.nbl[:, a]))
            wr[("nbl", a)] = [("anb%d" % a, n)]
        g.remote_dma_fused(trs, local_sem=T.sem.sent)
        sent[0] += len(far)

    packets(1)
    summed(1, 2)
    summed(2, 4)
    single(1)
    lists(1)
    packets(2)
    summed(0, 1)
    single(2)
    single(3)
    lists(2, 3)
    packets(3)
    op("v", lambda: V.tensor_copy(T.town[:, 3072:4096], T.town[:, 0:1024]), [("to", 0)], [("to", 1)])
    single(0)

    wr[("nbl", 0)] = wr[("nbs", 0)]
    for what, a in TURNS:
        if what == "n":
            copies("y", [(T.nbr[32 * a:32 * a + 32], T.nbl[:, a, 0:128])], "tnb", [("nbl", a)], ("nbr", a))
            wr["nbr"] = wr[("nbr", a)]
        else:
            copies("y", [(T.pkr[32 * a:32 * a + 32, 512 * j:512 * j + 512], T.pkl[32 * j:32 * j + 32, 512 * a:512 * a + 512])
                         for j in range(4)] if a else [(T.pkr[0:32, :], T.packets[32 * rank:32 * rank + 32, :])],
                   "tpk", [("pkl", a)], ("pkr", a))
            wr["pkr"] = wr[("pkr", a)]

    op("s", [lambda: A.activation(T.col[:, 1:2], T.col[:, 0:1], ACT.Identity, scale=-3.0, bias=-3 * M),
             lambda: A.activation(T.tt[:, 4:8], T.mk[:, 4:8], ACT.Identity, scale=-24576.0, accum_out=T.col[:, 2:3]),
             lambda: A.activation(T.tt[:, 0:4], T.mk[:, 0:4], ACT.Identity, scale=X0 - X, bias=X / 4, accum_out=T.col[:, 4:5]),
             lambda: A.activation(T.cap[:], T.mk[:, 0:4], ACT.Identity, scale=256 - 1e6, bias=1e6),
             lambda: A.activation(T.bia[:], T.mk[:, 0:4], ACT.Identity, scale=256.0),
             lambda: A.activation(T.flip[:], T.mk[:, 0:4], ACT.Identity, scale=-2.0, bias=1.0),
             lambda: A.activation(T.scl[:], T.mk[:, 0:4], ACT.Identity, scale=2.0, bias=-1.0)], ["mk", "low"], ["col", ("t", 0)])
    scatter1(0)
    op("v", lambda: V.tensor_scalar(T.pi0[:, 0:1], T.pi0[:, 16:17], 63, None, ALU.bitwise_and), [], ["pi0"])
    op("v", lambda: V.tensor_scalar(T.col[:, 6:7], T.pi0[:, 0:1], 16.0, 3 * (M - M0), ALU.is_lt, ALU.mult), ["pi0"], ["end0"])

    def fill(ap, n, x):
        return lambda: A.activation(ap, T.ones[:, 0:n], ACT.Copy, scale=x)

    op("s", [fill(T.zz[:, 0:3], 432, 0.0), fill(T.zz[:, 3:6], 432, 0.0)], ["ones"], ["zz"])
    op("s", [fill(T.tm[:, S:S + 16], 16, 0.0), fill(ps[5][:, 4:160:5], 32, 0.0), fill(ps[6][:, 4:160:5], 32, 0.0),
             fill(T.nbc[:, 4:640:5], 128, 2 * C), fill(T.half[:], 128, 0.5),
             lambda: A.activation(T.dig[:, 9], T.ones[:, 0:128], ACT.Identity, scale=T.col[:, 3:4])], ["ones", "mk"],
       ["tmz", ("ps", 5), ("ps", 6), "nb5", "half", ("dig", 9)])

    def later():
        op("s", [lambda o=o, n=n: A.activation(T.town[:, CB + o:CB + o + n], T.ones[:, 0:n], ACT.Identity, scale=T.col[:, 2:3])
                 for o, n in ((0, 512), (512, CAP - 512))] +
           [fill(T.eight[:], 32, 8.0), fill(T.sgn[:, 0:8], 8, -1.0), lambda: A.activation(T.pd[:], T.ident[:], ACT.Copy, scale=BIG / 2),
            lambda: A.activation(T.col[:, 5:6], T.col[:, 6:7], ACT.Identity, bias=-3 * M)],
           ["col", "ident", "end0"], ["left", "eight", "sgn", "pd", "end"])

    op("g", lambda: g.affine_select(T.ident[:], T.ones[:, 0:128], [[-1, 128]], ALU.is_equal, 0.0, 0, 1), ["ones"], ["ident"])
    for b in range(4):
        op("g", lambda: g.affine_select(T.wm[32 * b:32 * b + 32, :], T.ones[32 * b:32 * b + 32, 0:128], [[0, 4], [-1, 32]],
                                        ALU.is_equal, 0.0, 0, 1), ["ones"], ["wm"])
    for x0, x1, at, w in ([(0, 1, k, WK[k]) for k in range(5)] + [(1, 5, 4, -1.0), (1, 5, 8, 1.0), (5, 6, 12, -16.0), (5, 6, 13, -1.0)]):
        z = T.zz[:, x0:x1, 15:128:16]
        op("g", lambda: g.affine_select(z, z, [[-1, x1 - x0], [-16, 8]], ALU.not_equal, w, -at, 1), [], ["zz"])
    op("g", [lambda h=h: g.iota(T.gate[:, 160 * h:160 * h + 160], [[16, 32], [-32000, 5]], int(C) + (S, DB)[h], 1,
                                allow_small_or_imprecise_dtypes=True) for h in range(2)], [], ["gate"])
    op("g", lambda: g.iota(T.dig[:, 8], [[-1, 128]], 0, 0, allow_small_or_imprecise_dtypes=True), [], [("dig", 8)])
    op("s", [lambda: A.activation(T.diag[:, 0:128], T.ident[:], ACT.Copy, scale=-1.0),
             lambda: A.activation(T.id32[:], T.ident[:], ACT.Copy)] +
       [lambda k=k: A.activation(T.diag[:, 128 * k + 128:128 * k + 256], T.ident[:], ACT.Identity, scale=T.scl[:, k:k + 1])
        for k in range(4)] + [lambda: A.activation(T.diag[:, 640:768], T.ident[:], ACT.Identity, scale=T.col[:, 4:5]),
                              lambda: A.activation(T.col[:, 7:8], T.col[:, 4:5], ACT.Identity, bias=-127.5)],
       ["ident", "col"], ["diag"])
    op("s", [fill(T.pay0[:, 512 * b:512 * b + 512], 512, 0.0) for b in (1, 2, 3)], ["ones"], ["pay0"])

    def digits(b):
        op("s", [lambda k=k: A.activation(T.dig[:, k], T.nbc[:, k:640:5], ACT.Identity, bias=-64.0, scale=-1.0) for k in range(4)],
           ["nbc"], [("dig", 0)])
        op("p", [f for k in range(4) for f in
                 (lambda k=k: PE.matmul(ps[b][:, 128 * k:128 * k + 128], T.id32[:], T.nbc[:, k:640:5], True, False),
                  lambda k=k: PE.matmul(ps[b][:, 128 * k:128 * k + 128], T.ident[:], T.dig[:, k], False, True))],
           ["nbc", ("dig", 0), "ident", "diag"], [("ps", b)])

    def payload(b):
        op("s", lambda: A.activation(T.dig[:, 4:8], ps[b][:], ACT.Copy), [], [("ps", b), ("dig", 4)])
        copies("y", [(T.pay0[4 + d:128:16, :], T.dig[:, d]) for d in range(10)], "tpay", [("dig", d) for d in (0, 4, 8, 9)], "pay0")
        op("g", [lambda r=r: g.affine_select(T.pay[:, r:P:16], T.pay0[:, 128 * r:128 * r + 128], [[0, 128]], ALU.is_ge, 0.0, 0, 0)
                 for r in range(16)], ["pay0"], ["pay"])
        for b in range(4):
            op("g", lambda: g.affine_select(T.lfin[32 * b:32 * b + 32, :], T.ones[32 * b:32 * b + 32, :], [[1, 4], [-1, 128]],
                                            ALU.is_equal, 0.0, 0, 4), ["ones"], ["lfin"])

    scatter1(1)
    scatter1(2)
    scatter1(3)
    op("g", lambda: g.affine_select(T.bd0[:], T.half[:], [[-16, 8], [0, 16]], ALU.is_ge, 0.0, 0, 1), ["half"], ["bd0"])
    op("g", lambda: g.affine_select(T.bd[:], T.bd0[:], [[16, 8], [0, 16]], ALU.is_ge, 0.0, 15, -1), ["bd0"], ["bd"])
    op("g", lambda: g.affine_select(T.pb[:], T.bd[:], [[-1, 128]], ALU.is_ge, 0.0, 0, 1), ["bd"], ["pb"])
    op("g", lambda: g.affine_select(T.pa0[:], T.bd[:], [[1, 128]], ALU.is_gt, 0.0, 0, -1), ["bd"], ["pa0"])
    op("g", lambda: g.affine_select(T.pa[:], T.pa0[:], [[-1, 128]], ALU.not_equal, -BIG / 2, 0, 1), ["pa0"], ["pa"])

    TM = [("tm", b) for b in range(16)] + ["tmz"]
    bank = [0]

    def merge(between=(), who="sv" * 8):
        for b in range(16):
            k = bank[0] % 5
            bank[0] += 1
            op("p", lambda: PE.matmul(ps[k][:], T.wm[:], T.town[:, 512 * b:512 * b + 512], True, True), TO + ["wm"], [("ps", k)])
            if who[b] == "s":
                op("s", lambda: A.activation(T.tm[:, 512 * b:512 * b + 512], ps[k][:], ACT.Identity, bias=T.col[:, 1:2]),
                   ["col"], [("ps", k), ("tm", b)])
            else:
                op("v", lambda: V.tensor_scalar(T.tm[:, 512 * b:512 * b + 512], ps[k][:], T.col[:, 1:2], None, ALU.add),
                   ["col"], [("ps", k), ("tm", b)])
            if b in between:
                between[b]()

    def flags(t):
        copies("y", [(T.fl[32 * a:32 * a + 32, 128 * t:128 * t + 128], T.tm[0:32:16, P * dst[a]:P * dst[a] + P]) for a in range(NR)],
               "tfl", TM, "fl")
        for b in TM:
            rd[b] = rd.get(b, []) + wr["fl"]

    def unwrap(k, o, x):
        op("p", [lambda r=r: PE.matmul(ps[k][:, o:o + 48], T.zz[:, x, 15 - r:143 - r], T.town[:, CB + r:DB:16], r == 0, r == 15)
                 for r in range(16)], ["left", "zz"], [("ps", k)])

    def numbers():
        op("v", lambda: V.tensor_copy(T.nb4[:, 4], ps[5][:, 320:368]), [], [("ps", 5), ("nb4", 4)])
        op("s", lambda: A.activation(T.pk4[:], T.pkr[:].indirect(T.nb4[:, 4]), ACT.Copy), ["pkr", ("nb4", 4)], ["pk4"])

    def places(h):
        op("v", lambda: V.tensor_scalar(T.nb4[:, 2 * h:2 * h + 2], ps[6 - h][:, 368:464], -C, None, ALU.add), [],
           [("ps", 6 - h), ("nb4", 2 * h), ("nb4", 2 * h + 1)])

    def peel(t):
        chunks, order = ROUND[t]
        steps = [(x[0], int(x[1])) for x in order.split()]
        ends = [i for c, i in steps if c == "d"]
        win = T.tm[:, 0:S + 1]
        pk = T.pk4 if t == 4 else T.pkr
        held = {i: [] for i in range(len(chunks))}
        done = {i: [] for i in range(len(chunks))}
        free, xb, zb = [0, 1, 2, 3], {}, {}
        flags(t - 2)
        for c, i in steps:
            if c in "oune":
                if c == "o":
                    rounds_out(i)
                elif c == "e":
                    (lambda: digits(7), lambda: payload(7), later)[i]()
                elif t == 2:
                    op("v", [lambda k=k: V.tensor_scalar(T.nbc[:, k:640:5], T.nbr[:, k], C, None, ALU.add) for k in range(4)], ["nbr"], ["nbc"])
                elif c == "u":
                    places(1)
                else:
                    op("s", [lambda k=k: A.activation(T.nbc[:, k:240:5], ps[6 - k // 2][:, 368 + 48 * (k % 2):416 + 48 * (k % 2)], ACT.Copy)
                             for k in range(4)] + [fill(T.nbc[:, 4:240:5], 48, 2 * C)], [], [("ps", 5), ("ps", 6), "nbc", "nb5"])
                continue
            h = min(n for n, e in enumerate(ends) if e >= i)
            b0 = chunks[ends[h - 1]][1] if h else 0
            c0, c1 = (b0, chunks[i][1]) if c in "dpabcs" else chunks[i]
            u, w, m, o, e = 16 * c0, 16 * (c1 - c0), c1 - c0, 5 * c0, 5 * c1
            h %= 2
            f, st, dd = ps[4][:, 64 * h + c0 - b0:64 * h + c1 - b0], ps[4][:, 128 + 64 * h:128 + 64 * h + m], ps[5 + h]
            F, D = ("ps", 4), ("ps", 5 + h)
            if i not in xb and (c in "0123" or len(held[i]) == 3):
                xb[i] = free.pop(0)
            if i in xb and c not in "dpabcs":
                x, B = ps[xb[i]][:, 0:w], ("ps", xb[i])

            def keys(name):
                return [(name, cc) for cc in range(c0, c1, 4)]

            def place(k, last):
                sign = 0 if ("vwxy"[k], i) in steps else k + 1
                return lambda: PE.matmul(x, T.diag[:, 128 * sign:128 * sign + 128], T.gat[:, P * k + u:P * k + u + w], False, last)

            def first(lift):
                return ([lambda: PE.matmul(x, T.ident[:], pk[:, u:u + w], True, False)] +
                        [lambda: PE.matmul(x, T.diag[:, 640:768], T.ones[:, 0:w], False, False)] * lift)

            def less():
                done[i].append(c)
                if len(done[i]) == 6:
                    xb[i] = zb[i]
                    op("p", lambda: PE.matmul(ps[xb[i]][:, 0:w], T.diag[:, 0:128], T.qq[:, u:u + w], False, True), keys("q"), [("ps", xb[i])])

            if c in "vwxy0123":
                k = "vwxy0123".index(c) % 4
                out = T.gat[:, P * k + u:P * k + u + w]
                lst, key = (T.nb4[:, k, c0:c1], ("nb4", k)) if t == 4 else (T.nbr[:, k, c0:c1], "nbr")
                if c in "vwxy":
                    op("v", lambda: V.tensor_scalar(out, win.indirect(lst), T.cap[:, k:k + 1], None, ALU.min), TM + [key, "col"], keys(("g", k)))
                else:
                    op("s", lambda: A.activation(out, win.indirect(lst), ACT.Relu, bias=T.bia[:, k:k + 1], scale=T.flip[:, k:k + 1]),
                       TM + [key, "col"], keys(("g", k)))
                held[i].append(k)
                if c not in "vwxy" or len(done[i] + held[i]) == 4:
                    if not done[i]:
                        op("p", first(("z", i) not in steps), ["pk4" if t == 4 else "pkr", "ident", "diag"], [B])
                    for kk in held[i]:
                        done[i].append(kk)
                        op("p", place(kk, len(done[i]) == 4), keys(("g", kk)) + ["diag"], [B])
                    held[i] = []
            elif c in "qQ":
                bias = T.col[:, 7:8] if ("z", i) in steps else -127.5
                if c == "q":
                    op("s", lambda: A.activation(T.qq[:, u:u + w], x, ACT.Relu, bias=bias), ["diag"], [B] + keys("q"))
                else:
                    op("v", lambda: V.tensor_scalar(T.qq[:, u:u + w], x, bias, 0.0, ALU.add, ALU.max), ["diag"], [B] + keys("q"))
                op("p", [lambda r=r: PE.matmul(f, T.zz[:, 0, 15 - r:143 - r], T.qq[:, u + r:u + w:16], r == 0, r == 15)
                         for r in range(16)], keys("q") + ["zz"], [F])
                if ("z", i) in steps:
                    free.append(xb[i])
                    less()
            elif c == "d":
                if t == 3:
                    op("s", lambda: A.activation(T.sgn[:, 8 + c0:8 + c1], f, ACT.Sign, bias=TWO, scale=-1.0), [], [F, "sgn"])
                op("s", [lambda k=k: A.activation(dd[:, k:5 * m:5], f, ACT.Abs, bias=-LAM[k]) for k in range(4)], [], [F, D])
                if t == 3:
                    op("p", [lambda: PE.matmul(st, T.pa[:], T.sgn[:, 8 + c0:8 + c1], True, False),
                             lambda: PE.matmul(st, T.pb[:], T.sgn[:, 7 + c0:7 + c1], False, False),
                             lambda: PE.matmul(st, T.pd[:], T.sgn[:, 7 + c0:7 + c1], False, True)],
                       ["sgn", "pa", "pb", "pd"], [F])
            elif c == "z":
                zb[i] = free.pop(0)
                x, B = ps[zb[i]][:, 0:w], ("ps", zb[i])
                op("p", first(True) + [place(kk, False) for kk in range(4)], [y for kk in range(4) for y in keys(("g", kk))], [B])
                less()
            elif c == "r":
                if i not in zb:
                    op("v", lambda: V.tensor_tensor(x if t == 3 else T.rr[:, u:u + w], x, T.qq[:, u:u + w], ALU.subtract),
                       keys("q"), [B] + keys("r"))
                if t == 3:
                    op("v", lambda: V.tensor_tensor(T.rr[:, u:u + w], x, T.pay[:, u:u + w], ALU.max), ["pay"], [B] + keys("r"))
                elif i in zb:
                    op("s", lambda: A.activation(T.rr[:, u:u + w], x, ACT.Copy), [], [B] + keys("r"))
                free.append(xb[i])
            elif c == "s":
                op("v", lambda: V.tensor_copy(T.town[:, 0:TW if t == 3 else CB].indirect(T.offs[:, c0:c1]), T.rr[:, u:u + w]),
                   keys("offs") + keys("r"), TO + ["left"] * (t == 3))
            elif c == "p":
                op("v", lambda: V.tensor_tensor_scan(T.nbc[:, o + 4:e:5], st, T.eight[:, 0:m],
                                                     T.nbc[:, o - 1:o] if c0 else C + CB + BIG, ALU.add, ALU.add),
                   ["eight"], [F, "nb5"])
            elif c == "a":
                op("v", lambda: V.tensor_tensor(T.tt[:, o:e], dd[:, 0:5 * m], T.nbc[:, o:e], ALU.max), ["nbc", "nb5"], [D] + keys("t"))
            elif c == "b":
                op("v", lambda: V.tensor_tensor_scan(T.scn[:, o:e], T.gate[:, 160 * (t == 3):160 * (t == 3) + 5 * m], T.tt[:, o:e], 0.0, ALU.max, ALU.min),
                   keys("t") + ["gate"], keys("sc"))
            else:
                op("v", lambda: V.tensor_scalar(T.offs[:, c0:c1], T.scn[:, o + 4:e:5], -C, None, ALU.add), keys("sc"), keys("offs"))

    def rounds_out(half):
        if half == 0:
            op("s", lambda: A.activation(T.sg[:], T.fl[:], ACT.Sign, bias=-1000.0), ["fl"], ["sg"])
            op("p", [lambda t=t: PE.matmul(ps[7][:, 384:512], T.sg[:, 128 * t:128 * t + 128], T.ident[:], t == 0, t == 2)
                     for t in range(3)], ["sg", "ident"], [("ps", 7)])
        else:
            op("s", lambda: A.activation(T.ys[:, :, 512:544], ps[7][:, 384:512], ACT.Identity, bias=2.5, scale=0.5), [], [("ps", 7), "rs"])

    merge()
    peel(2)
    merge()
    peel(3)
    merge(dict(zip(LAST[0], (lambda: unwrap(5, 320, 5), numbers, lambda: unwrap(6, 368, 1), lambda: unwrap(6, 416, 2), lambda: places(0)))),
          LAST[1])
    unwrap(5, 368, 3)
    unwrap(5, 416, 4)
    peel(4)

    stored = [0]

    def store(e, out, in_, reads):
        deps(e, reads, [])
        Q[e].dma_start(out, in_).then_inc(T.sem.stored, 16)
        stored[0] += 16

    def rounds_in(a):
        op("p", lambda: PE.matmul(ps[4 + a][0:32, 0:128], (T.yl if a else T.ys)[:, a, 512:544], T.ident[:], True, True),
           [("yl", a) if a else "rs"], [("ps", 4 + a)])
        op("v", lambda: V.tensor_copy(T.rf[0:32, 128 * a:128 * a + 128], ps[4 + a][0:32, 0:128]), [], [("ps", 4 + a), ("rf", a)])
        store("s", T.rounds[2 * src[a]:2 * src[a] + 2, :], T.rf[0:32, 128 * a:128 * a + 128], [("rf", a)])

    for i, a in enumerate((1, 2, 3, 0)):
        o = P * dst[a]
        for h in range(2):
            k, u = (2 * i + h) % 4, 256 * h
            op("p", [lambda j=j: PE.matmul(ps[k][:, 0:256], T.lfin[:, 128 * j:128 * j + 128], T.town[:, o + 512 * j + u:o + 512 * j + u + 256],
                                           j == 0, j == 3) for j in range(4)], TO + ["lfin"], [("ps", k)])
            out = T.ys[:, a, u:u + 256] if a else T.yf[:, u:u + 256]
            if h:
                op("v", lambda: V.tensor_scalar(out, ps[k][:, 0:256], T.col[:, 5:6], None, ALU.add), ["end"], [("ps", k), ("ys", a, h)])
            else:
                op("s", lambda: A.activation(out, ps[k][:, 0:256], ACT.Identity, bias=T.col[:, 5:6]), ["end"], [("ps", k), ("ys", a, h)])
        if a:
            send(a, T.yl[:, a], T.ys[:, a], "ay%d" % a, [("ys", a, 0), ("ys", a, 1), "rs"], ("yl", a))
        else:
            store("y", T.y[32 * rank:32 * rank + 32, :], T.yf[:, 0:512], [("ys", a, 0), ("ys", a, 1)])
    rounds_in(0)
    for a in (1, 2, 3):
        o = 512 * a
        op("v", lambda: V.tensor_copy(T.yf[:, o:o + 256], T.yl[:, a, 0:256]), [("yl", a)], [("yf", a, 0)])
        op("s", lambda: A.activation(T.yf[:, o + 256:o + 512], T.yl[:, a, 256:512], ACT.Copy), [("yl", a)], [("yf", a, 1)])
        store("y", T.y[32 * src[a]:32 * src[a] + 32, :], T.yf[:, o:o + 512], [("yf", a, 0), ("yf", a, 1)])
        rounds_in(a)
    g.sync.wait_ge(T.sem.stored, stored[0])
    g.wait_ge(T.sem.sent, sent[0])
    for e in CS:
        wait("g", (CS[e], cnt[e]))
